import numpy as np
import ml_dtypes


def mxq(x, axis, fmt="e4m3"):
    dtype, down = {"e4m3": (ml_dtypes.float8_e4m3fn, 7), "e5m2": (ml_dtypes.float8_e5m2, 14)}[fmt]
    v = np.moveaxis(np.asarray(x, np.float32).astype(ml_dtypes.bfloat16).astype(np.float64), axis, -1)
    blocks = v.reshape(v.shape[:-1] + (-1, 32))
    amax = np.abs(blocks).max(-1, keepdims=True)
    byte = np.maximum(np.where(amax > 0, np.frexp(amax)[1] - 1 + 127, 0) - down, 1)
    scale = np.exp2(byte - 127.0)
    codes = (blocks / scale).astype(np.float32).astype(dtype).astype(np.float64)
    return np.moveaxis((codes * scale).reshape(v.shape), -1, axis)


WIDE = False


def mx_kscale(k):
    if not WIDE:
        return np.ones(k)
    levels = np.array([30, -30])
    if k % 512:
        return np.exp2(np.random.permutation(np.resize(levels, k // 32))).repeat(32)
    a = np.empty((k // 512, 16))
    for p in range(k // 512):
        a[p, :8] = np.random.permutation(np.resize(levels, 8))
        for g in range(8):
            far = levels[np.abs(levels - a[p, g]) >= 10]
            a[p, g + 8] = far[np.random.randint(len(far))]
    return np.exp2(a.ravel()).repeat(32)


def f64(x):
    return np.asarray(x).astype(np.float64)


E2M1 = np.array([0.0, 0.5, 1.0, 1.5, 2.0, 3.0, 4.0, 6.0, -0.0, -0.5, -1.0, -1.5, -2.0, -3.0, -4.0, -6.0])


def pack_weight(w, fmt):
    k, n = w.shape
    w = f64(np.asarray(w, np.float32).astype(ml_dtypes.bfloat16)).reshape(k // 32, 32, n)
    amax = np.abs(w).max(1)
    if fmt == "e4m3":
        byte = np.frexp(amax)[1] - 1 + 127 - 7
    else:
        mant, ex = np.frexp(amax / 6.0)
        byte = np.where(mant > 0.5, ex, ex - 1) + 127
    byte = np.clip(np.where(amax > 0, byte, 1), 1, 254)
    scaled = (w * np.exp2(127.0 - byte)[:, None, :]).reshape(k, n).astype(np.float32)
    by_word = np.ascontiguousarray(scaled.reshape(k // 512, 128, 4, n).transpose(0, 1, 3, 2))
    if fmt == "e4m3":
        words = by_word.astype(ml_dtypes.float8_e4m3fn).view(np.uint8)
    else:
        c = by_word.astype(ml_dtypes.float4_e2m1fn).view(np.uint8) & 0xF
        words = (c[..., 0::2] | (c[..., 1::2] << 4)).reshape(k // 512, 128, 2 * n)
    return np.ascontiguousarray(words), np.ascontiguousarray(byte.astype(np.uint8).reshape(k // 512, 16, n))


def unpack_weight(words, scales, fmt):
    g, _, n = scales.shape
    words = np.ascontiguousarray(words).reshape(g, 128, n, -1)
    if fmt == "e4m3":
        vals = words.view(ml_dtypes.float8_e4m3fn).astype(np.float64)
    else:
        nib = np.empty((g, 128, n, 4), np.uint8)
        nib[..., 0::2] = words & 0xF
        nib[..., 1::2] = words >> 4
        vals = E2M1[nib]
    vals = vals * np.repeat(np.exp2(scales.astype(np.float64) - 127.0), 8, axis=1)[..., None]
    return vals.transpose(0, 1, 3, 2).reshape(g * 512, n)


K, O, T, R, N = 1024, 1024, 1024, 512, 1536


def setup_inputs():
    n = np.random.standard_normal
    s = mx_kscale(K)[:, None]
    u = mx_kscale(T)[:, None]
    m = np.exp(0.5 * n((O + T, 1)))
    ux = mx_kscale(O)[:, None]
    p_hs = pack_weight(n((O, R)) * ux, "e2m1")
    return {
        "x": (n((K, T)) * s * u.T).astype(np.float32),
        "dn": (n((K, R)) / np.sqrt(K) / s).astype(np.float32),
        "hs_words": p_hs[0],
        "hs_scales": p_hs[1],
        "dy0": (m[:O] * n((O, N)) / np.sqrt(O + T) / ux).astype(np.float32),
        "dy1": (m[O:] * n((T, N)) / np.sqrt(O + T) / u).astype(np.float32),
        "prm": (0.1 * n((R, N))).astype(np.float32),
    }


def reference(x, dn, hs_words, hs_scales, dy0, dy1, prm):
    x_ = mxq(f64(x), 0, "e4m3")
    dn_ = mxq(f64(dn), 0, "e4m3")
    h = x_.T @ dn_
    h_ = mxq(h, 0, "e4m3")
    hs_ = unpack_weight(hs_words, hs_scales, "e2m1")
    dy0_ = mxq(f64(dy0), 0, "e5m2")
    dy1_ = mxq(f64(dy1), 0, "e5m2")
    db = hs_.T @ dy0_ + h_.T @ dy1_
    return f64(prm) - 0.0625 * db

@@ -1,0 +1,225 @@
+from contextlib import ExitStack
+
+import concourse.mybir as mybir
+
+K, O, T, R, N = 1024, 1024, 1024, 512, 1536
+FLOPS = 2 * K * T * R + 2 * (O + T) * R * N
+STEP = -0.0625
+
+F32 = mybir.dt.float32
+BF16 = mybir.dt.bfloat16
+I32 = mybir.dt.int32
+U32 = mybir.dt.uint32
+U8 = mybir.dt.uint8
+E4M3 = mybir.dt.float8_e4m3fn_x4
+E5M2 = mybir.dt.float8_e5m2_x4
+E2M1 = mybir.dt.float4_e2m1fn_x4
+ALU = mybir.AluOpType
+
+P = 128
+PACK = 4
+PASS = P * PACK
+BLK = 512
+BANKS = 8
+V_COLS = 320
+V_COLS_LAST = 256
+
+
+def tile_mix_lorab_sgd_kernel(tc, x, dn, hs_words, hs_scales, dy0, dy1, prm, out):
+    nc = tc.nc
+    n_blocks = N // BLK
+    r_tiles = R // P
+
+    with ExitStack() as ctx:
+        raw = ctx.enter_context(tc.tile_pool(name="raw", bufs=4))
+        keep = ctx.enter_context(tc.tile_pool(name="keep", bufs=1))
+        stage = ctx.enter_context(tc.tile_pool(name="stage", bufs=6))
+        psum = ctx.enter_context(tc.psum_pool(name="psum", bufs=1))
+        ctx.enter_context(tc.manual_schedule())
+
+        def load_pass(src, a, name):
+            width = src.shape[1]
+            t = raw.tile([P, PACK, width], F32, name=name, tag="raw")
+            nc.sync.dma_start(out=t[:], in_=src[a * PASS : (a + 1) * PASS, :].rearrange("(p j) w -> p j w", j=PACK))
+            return t
+
+        def planes(name, width):
+            codes = keep.tile([P, width], U32, name=name + "_codes", align_bytes=64)
+            scales = keep.tile([P, width], U8, name=name + "_scales", align_bytes=64)
+            return codes, scales
+
+        def staged(name):
+            return stage.tile([P, BLK, PACK], BF16, name=name, tag="stage", align_bytes=64)
+
+        def copy_on(engine, dst, src):
+            if engine == "vector":
+                nc.vector.tensor_copy(out=dst, in_=src)
+            else:
+                nc.scalar.copy(out=dst, in_=src)
+
+        def interleave(engine, dst, src):
+            copy_on(engine, dst.rearrange("p (c i) j -> p c j i", i=4), src.rearrange("p j (c i) -> p c j i", i=4))
+
+        def quantize(g, plane, col0, fmt):
+            codes, scales = plane
+            nc.vector.quantize_mx(
+                out=codes[:, col0 : col0 + BLK].bitcast(fmt),
+                scales=scales[:, col0 : col0 + BLK],
+                in_=g[:].rearrange("p w j -> p (w j)"),
+            )
+
+        def bank_tile(i, name):
+            return psum.tile([P, BLK], F32, name=name, tag="bank%d" % i)
+
+        hs_sc = keep.tile([P, 2, R], U8, name="hs_sc", align_bytes=64)
+        nc.gpsimd.memset(hs_sc[:].bitcast(U32), 0)
+        for q in range(4):
+            nc.gpsimd.dma_start(
+                out=hs_sc[32 * q : 32 * q + 4, :, :].bitcast(I32),
+                in_=hs_scales[:, 4 * q : 4 * q + 4, :].rearrange("a r n -> r a n").bitcast(I32),
+            )
+
+        x_raw = [load_pass(x, 0, "x_raw0")]
+        dn_raw = keep.tile([P, 2, PACK, R], F32, name="dn_raw")
+        nc.sync.dma_start(
+            out=dn_raw[:].rearrange("p a j r -> p a (j r)"), in_=dn.rearrange("(a p j) r -> p a (j r)", a=2, j=PACK)
+        )
+        x_raw.append(load_pass(x, 1, "x_raw1"))
+        hs_w = keep.tile([P, 2, 2 * R], U8, name="hs_w", align_bytes=64)
+        nc.sync.dma_start(out=hs_w[:].bitcast(I32), in_=hs_words.rearrange("a p w -> p a w").bitcast(I32))
+        dy_raw = [load_pass(dy0, 0, "dy_raw0"), load_pass(dy0, 1, "dy_raw1")]
+
+        x_q = [planes("x%d" % a, T) for a in range(2)]
+        dn_q = [planes("dn%d" % a, R) for a in range(2)]
+        h_q = [planes("h%d" % b, R) for b in range(2)]
+        dy_q = [planes("dy%d" % g, N) for g in range(4)]
+
+        def x_pass(a):
+            gs = []
+            for b, engine in enumerate(("vector", "scalar")):
+                g = staged("x_g%d%d" % (a, b))
+                copy_on(
+                    engine,
+                    g[:].rearrange("p (t m) j -> p m j t", t=4),
+                    x_raw[a][:, :, b * BLK : (b + 1) * BLK].rearrange("p j (m t) -> p m j t", t=4),
+                )
+                gs.append(g)
+            for b in range(2):
+                quantize(gs[b], x_q[a], b * BLK, E4M3)
+
+        x_pass(0)
+        dn_g = []
+        for a, engine in enumerate(("vector", "scalar")):
+            g = staged("dn_g%d" % a)
+            interleave(engine, g[:], dn_raw[:, a, :, :])
+            dn_g.append(g)
+        for a in range(2):
+            quantize(dn_g[a], dn_q[a], 0, E4M3)
+        x_pass(1)
+
+        dy_raw.append(load_pass(dy1, 0, "dy_raw2"))
+        last_rows = dy1[PASS:, :].rearrange("(p j) w -> p j w", j=PACK)
+        halves = []
+
+        def load_half(u):
+            t = raw.tile([P, 2, N], F32, name="dy_half%d" % u, tag="raw")
+            nc.sync.dma_start(out=t[:], in_=last_rows[:, 2 * u : 2 * u + 2, :])
+            halves.append(t)
+
+        load_half(0)
+
+        h_g = []
+        for b in range(2):
+            g = staged("h_g%d" % b)
+            for rt in range(r_tiles):
+                bank = bank_tile(b * r_tiles + rt, "h_bank%d%d" % (b, rt))
+                for j in range(PACK):
+                    tc0 = b * BLK + j * P
+                    for a in range(2):
+                        nc.tensor.matmul_mx(
+                            out=bank[:, j * P : (j + 1) * P],
+                            lhsT=x_q[a][0][:, tc0 : tc0 + P].bitcast(E4M3),
+                            lhsT_scale=x_q[a][1][:, tc0 : tc0 + P],
+                            rhs=dn_q[a][0][:, rt * P : (rt + 1) * P].bitcast(E4M3),
+                            rhs_scale=dn_q[a][1][:, rt * P : (rt + 1) * P],
+                            start=(a == 0),
+                            stop=(a == 1),
+                        )
+                nc.scalar.copy(out=g[:, rt * P : (rt + 1) * P, :], in_=bank[:].rearrange("p (j r) -> p r j", j=PACK))
+            h_g.append(g)
+
+        tiles = [(rt, nb) for rt in range(r_tiles) for nb in range(n_blocks)]
+        early, late = tiles[:BANKS], tiles[BANKS:]
+        acc = {}
+        for i, key in enumerate(early):
+            acc[key] = bank_tile(i, "acc%d%d" % key)
+
+        def db_pass(key, g):
+            rt, nb = key
+            if g < 2:
+                lhsT = hs_w[:, g, 2 * P * rt : 2 * P * (rt + 1)].bitcast(E2M1)
+                lhsT_scale = hs_sc[:, g, P * rt : P * (rt + 1)]
+            else:
+                lhsT = h_q[g - 2][0][:, P * rt : P * (rt + 1)].bitcast(E4M3)
+                lhsT_scale = h_q[g - 2][1][:, P * rt : P * (rt + 1)]
+            nc.tensor.matmul_mx(
+                out=acc[key][:],
+                lhsT=lhsT,
+                lhsT_scale=lhsT_scale,
+                rhs=dy_q[g][0][:, nb * BLK : (nb + 1) * BLK].bitcast(E5M2),
+                rhs_scale=dy_q[g][1][:, nb * BLK : (nb + 1) * BLK],
+                start=(g == 0),
+                stop=(g == 3),
+            )
+
+        def copy_block(g_tile, src, nb, j0, v_cols):
+            nj = src.shape[1]
+            c0 = nb * BLK
+            interleave("vector", g_tile[:, :v_cols, j0 : j0 + nj], src[:, :, c0 : c0 + v_cols])
+            interleave("scalar", g_tile[:, v_cols:, j0 : j0 + nj], src[:, :, c0 + v_cols : c0 + BLK])
+
+        def finish_pass(g, gs, src, j0, v_cols):
+            def quantize_and_multiply(nb):
+                quantize(gs[nb], dy_q[g], nb * BLK, E5M2)
+                for key in early:
+                    if key[1] == nb:
+                        db_pass(key, g)
+
+            for nb in range(n_blocks):
+                copy_block(gs[nb], src, nb, j0, v_cols)
+                if nb > 0:
+                    quantize_and_multiply(nb - 1)
+            quantize_and_multiply(n_blocks - 1)
+
+        def dy_pass(g):
+            gs = [staged("dy_g%d%d" % (g, nb)) for nb in range(n_blocks)]
+            finish_pass(g, gs, dy_raw[g], 0, V_COLS)
+
+        dy_pass(0)
+        load_half(1)
+        prm_t = []
+        for rt in range(r_tiles):
+            t = keep.tile([P, N], F32, name="prm%d" % rt)
+            nc.sync.dma_start(out=t[:], in_=prm[rt * P : (rt + 1) * P, :])
+            prm_t.append(t)
+        for b in range(2):
+            quantize(h_g[b], h_q[b], 0, E4M3)
+        dy_pass(1)
+        dy_pass(2)
+        gs = [staged("dy_g3%d" % nb) for nb in range(n_blocks)]
+        for nb in range(n_blocks):
+            copy_block(gs[nb], halves[0], nb, 0, V_COLS_LAST)
+        finish_pass(3, gs, halves[1], 2, V_COLS_LAST)
+
+        for i, key in enumerate(tiles):
+            rt, nb = key
+            cols = slice(nb * BLK, (nb + 1) * BLK)
+            nc.vector.scalar_tensor_tensor(
+                out=prm_t[rt][:, cols], in0=acc[key][:], scalar=STEP, in1=prm_t[rt][:, cols], op0=ALU.mult, op1=ALU.add
+            )
+            if i < len(late):
+                acc[late[i]] = bank_tile(i, "acc%d%d" % late[i])
+                for g in range(4):
+                    db_pass(late[i], g)
+            if nb == n_blocks - 1:
+                nc.sync.dma_start(out=out[rt * P : (rt + 1) * P, :], in_=prm_t[rt][:])

@@ -122,8 +122,9 @@ def tile_mix_lorab_sgd_kernel(tc, x, dn, hs_words, hs_scales, dy0, dy1, prm, out
         halves = []
 
         def load_half(u):
-            t = raw.tile([P, 2, N], F32, name="dy_half%d" % u, tag="raw")
-            nc.sync.dma_start(out=t[:], in_=last_rows[:, 2 * u : 2 * u + 2, :])
+            c0, c1 = ((0, 2 * BLK), (2 * BLK, N))[u]
+            t = raw.tile([P, PACK, c1 - c0], F32, name="dy_half%d" % u, tag="raw")
+            nc.sync.dma_start(out=t[:], in_=last_rows[:, :, c0:c1])
             halves.append(t)
 
         load_half(0)
@@ -172,28 +173,23 @@ def tile_mix_lorab_sgd_kernel(tc, x, dn, hs_words, hs_scales, dy0, dy1, prm, out
                 stop=(g == 3),
             )
 
-        def copy_block(g_tile, src, nb, j0, v_cols):
-            nj = src.shape[1]
-            c0 = nb * BLK
-            interleave("vector", g_tile[:, :v_cols, j0 : j0 + nj], src[:, :, c0 : c0 + v_cols])
-            interleave("scalar", g_tile[:, v_cols:, j0 : j0 + nj], src[:, :, c0 + v_cols : c0 + BLK])
+        def copy_block(g_tile, src, c0, v_cols):
+            interleave("vector", g_tile[:, :v_cols, :], src[:, :, c0 : c0 + v_cols])
+            interleave("scalar", g_tile[:, v_cols:, :], src[:, :, c0 + v_cols : c0 + BLK])
 
-        def finish_pass(g, gs, src, j0, v_cols):
-            def quantize_and_multiply(nb):
-                quantize(gs[nb], dy_q[g], nb * BLK, E5M2)
-                for key in early:
-                    if key[1] == nb:
-                        db_pass(key, g)
-
-            for nb in range(n_blocks):
-                copy_block(gs[nb], src, nb, j0, v_cols)
-                if nb > 0:
-                    quantize_and_multiply(nb - 1)
-            quantize_and_multiply(n_blocks - 1)
+        def quantize_and_multiply(g, g_tile, nb):
+            quantize(g_tile, dy_q[g], nb * BLK, E5M2)
+            for key in early:
+                if key[1] == nb:
+                    db_pass(key, g)
 
         def dy_pass(g):
             gs = [staged("dy_g%d%d" % (g, nb)) for nb in range(n_blocks)]
-            finish_pass(g, gs, dy_raw[g], 0, V_COLS)
+            for nb in range(n_blocks):
+                copy_block(gs[nb], dy_raw[g], nb * BLK, V_COLS)
+                if nb > 0:
+                    quantize_and_multiply(g, gs[nb - 1], nb - 1)
+            quantize_and_multiply(g, gs[-1], n_blocks - 1)
 
         dy_pass(0)
         load_half(1)
@@ -207,9 +203,12 @@ def tile_mix_lorab_sgd_kernel(tc, x, dn, hs_words, hs_scales, dy0, dy1, prm, out
         dy_pass(1)
         dy_pass(2)
         gs = [staged("dy_g3%d" % nb) for nb in range(n_blocks)]
-        for nb in range(n_blocks):
-            copy_block(gs[nb], halves[0], nb, 0, V_COLS_LAST)
-        finish_pass(3, gs, halves[1], 2, V_COLS_LAST)
+        for nb in range(2):
+            copy_block(gs[nb], halves[0], nb * BLK, V_COLS_LAST)
+        for nb in range(2):
+            quantize_and_multiply(3, gs[nb], nb)
+        copy_block(gs[2], halves[1], 0, V_COLS_LAST)
+        quantize_and_multiply(3, gs[2], 2)
 
         for i, key in enumerate(tiles):
             rt, nb = key

@@ -21,8 +21,9 @@ PACK = 4
 PASS = P * PACK
 BLK = 512
 BANKS = 8
-V_COLS = 320
-V_COLS_LAST = 256
+V_COLS = 288
+V_COLS_PAIR = 256
+V_COLS_LAST = 384
 
 
 def tile_mix_lorab_sgd_kernel(tc, x, dn, hs_words, hs_scales, dy0, dy1, prm, out):
@@ -129,9 +130,8 @@ def tile_mix_lorab_sgd_kernel(tc, x, dn, hs_words, hs_scales, dy0, dy1, prm, out
 
         load_half(0)
 
-        h_g = []
-        for b in range(2):
-            g = staged("h_g%d" % b)
+        def h_products(b):
+            banks = []
             for rt in range(r_tiles):
                 bank = bank_tile(b * r_tiles + rt, "h_bank%d%d" % (b, rt))
                 for j in range(PACK):
@@ -146,17 +146,21 @@ def tile_mix_lorab_sgd_kernel(tc, x, dn, hs_words, hs_scales, dy0, dy1, prm, out
                             start=(a == 0),
                             stop=(a == 1),
                         )
-                nc.scalar.copy(out=g[:, rt * P : (rt + 1) * P, :], in_=bank[:].rearrange("p (j r) -> p r j", j=PACK))
-            h_g.append(g)
+                banks.append(bank)
+            return banks
 
-        tiles = [(rt, nb) for rt in range(r_tiles) for nb in range(n_blocks)]
-        early, late = tiles[:BANKS], tiles[BANKS:]
+        def h_quantize(b, banks, engine):
+            g = staged("h_g%d" % b)
+            for rt in range(r_tiles):
+                copy_on(engine, g[:, rt * P : (rt + 1) * P, :], banks[rt][:].rearrange("p (j r) -> p r j", j=PACK))
+            quantize(g, h_q[b], 0, E4M3)
+
+        h_banks = [h_products(b) for b in range(2)]
+        h_quantize(0, h_banks[0], "vector")
+
         acc = {}
-        for i, key in enumerate(early):
-            acc[key] = bank_tile(i, "acc%d%d" % key)
 
-        def db_pass(key, g):
-            rt, nb = key
+        def db_pass(rt, nb, g):
             if g < 2:
                 lhsT = hs_w[:, g, 2 * P * rt : 2 * P * (rt + 1)].bitcast(E2M1)
                 lhsT_scale = hs_sc[:, g, P * rt : P * (rt + 1)]
@@ -164,7 +168,7 @@ def tile_mix_lorab_sgd_kernel(tc, x, dn, hs_words, hs_scales, dy0, dy1, prm, out
                 lhsT = h_q[g - 2][0][:, P * rt : P * (rt + 1)].bitcast(E4M3)
                 lhsT_scale = h_q[g - 2][1][:, P * rt : P * (rt + 1)]
             nc.tensor.matmul_mx(
-                out=acc[key][:],
+                out=acc[rt, nb][:],
                 lhsT=lhsT,
                 lhsT_scale=lhsT_scale,
                 rhs=dy_q[g][0][:, nb * BLK : (nb + 1) * BLK].bitcast(E5M2),
@@ -173,52 +177,67 @@ def tile_mix_lorab_sgd_kernel(tc, x, dn, hs_words, hs_scales, dy0, dy1, prm, out
                 stop=(g == 3),
             )
 
+        def db_column(nb, g):
+            for rt in range(r_tiles):
+                db_pass(rt, nb, g)
+
         def copy_block(g_tile, src, c0, v_cols):
             interleave("vector", g_tile[:, :v_cols, :], src[:, :, c0 : c0 + v_cols])
             interleave("scalar", g_tile[:, v_cols:, :], src[:, :, c0 + v_cols : c0 + BLK])
 
-        def quantize_and_multiply(g, g_tile, nb):
-            quantize(g_tile, dy_q[g], nb * BLK, E5M2)
-            for key in early:
-                if key[1] == nb:
-                    db_pass(key, g)
-
-        def dy_pass(g):
+        def dy_pass(g, after_block):
             gs = [staged("dy_g%d%d" % (g, nb)) for nb in range(n_blocks)]
-            for nb in range(n_blocks):
-                copy_block(gs[nb], dy_raw[g], nb * BLK, V_COLS)
+            for nb in range(n_blocks + 1):
+                if nb < n_blocks:
+                    copy_block(gs[nb], dy_raw[g], nb * BLK, V_COLS)
                 if nb > 0:
-                    quantize_and_multiply(g, gs[nb - 1], nb - 1)
-            quantize_and_multiply(g, gs[-1], n_blocks - 1)
+                    quantize(gs[nb - 1], dy_q[g], (nb - 1) * BLK, E5M2)
+                    for key in after_block.get(nb - 1, []):
+                        db_column(*key)
 
-        dy_pass(0)
+        for rt in range(r_tiles):
+            acc[rt, 0] = bank_tile(rt, "acc%d0" % rt)
+        dy_pass(0, {0: [(0, 0)]})
         load_half(1)
         prm_t = []
         for rt in range(r_tiles):
             t = keep.tile([P, N], F32, name="prm%d" % rt)
             nc.sync.dma_start(out=t[:], in_=prm[rt * P : (rt + 1) * P, :])
             prm_t.append(t)
-        for b in range(2):
-            quantize(h_g[b], h_q[b], 0, E4M3)
-        dy_pass(1)
-        dy_pass(2)
+        h_quantize(1, h_banks[1], "scalar")
+        for rt in range(r_tiles):
+            acc[rt, 1] = bank_tile(r_tiles + rt, "acc%d1" % rt)
+        db_column(1, 0)
+        dy_pass(1, {1: [(1, 1)]})
+        dy_pass(2, {0: [(0, 1), (0, 2)], 1: [(1, 2)]})
+
         gs = [staged("dy_g3%d" % nb) for nb in range(n_blocks)]
         for nb in range(2):
-            copy_block(gs[nb], halves[0], nb * BLK, V_COLS_LAST)
-        for nb in range(2):
-            quantize_and_multiply(3, gs[nb], nb)
+            copy_block(gs[nb], halves[0], nb * BLK, V_COLS_PAIR)
+        leave_order = [1, 2, 0, 3]
+        quantize(gs[0], dy_q[3], 0, E5M2)
+        for rt in leave_order:
+            db_pass(rt, 0, 3)
+        quantize(gs[1], dy_q[3], BLK, E5M2)
         copy_block(gs[2], halves[1], 0, V_COLS_LAST)
-        quantize_and_multiply(3, gs[2], 2)
+        quantize(gs[2], dy_q[3], 2 * BLK, E5M2)
 
-        for i, key in enumerate(tiles):
-            rt, nb = key
-            cols = slice(nb * BLK, (nb + 1) * BLK)
-            nc.vector.scalar_tensor_tensor(
-                out=prm_t[rt][:, cols], in0=acc[key][:], scalar=STEP, in1=prm_t[rt][:, cols], op0=ALU.mult, op1=ALU.add
-            )
-            if i < len(late):
-                acc[late[i]] = bank_tile(i, "acc%d%d" % late[i])
-                for g in range(4):
-                    db_pass(late[i], g)
-            if nb == n_blocks - 1:
-                nc.sync.dma_start(out=out[rt * P : (rt + 1) * P, :], in_=prm_t[rt][:])
+        part = {}
+        for rt, left in enumerate(leave_order):
+            part[left] = keep.tile([P, BLK], F32, name="part%d" % left)
+            nc.scalar.mul(out=part[left][:], in_=acc[left, 0][:], mul=STEP)
+            acc[rt, 2] = bank_tile(left, "acc%d2" % rt)
+
+        for rt in range(r_tiles):
+            db_pass(rt, 1, 3)
+            for g in range(4):
+                db_pass(rt, 2, g)
+
+        for rt in range(r_tiles):
+            nc.gpsimd.tensor_tensor(out=prm_t[rt][:, :BLK], in0=part[rt][:], in1=prm_t[rt][:, :BLK], op=ALU.add)
+            for nb in range(1, n_blocks):
+                cols = slice(nb * BLK, (nb + 1) * BLK)
+                nc.vector.scalar_tensor_tensor(
+                    out=prm_t[rt][:, cols], in0=acc[rt, nb][:], scalar=STEP, in1=prm_t[rt][:, cols], op0=ALU.mult, op1=ALU.add
+                )
+            nc.sync.dma_start(out=out[rt * P : (rt + 1) * P, :], in_=prm_t[rt][:])

@@ -32,17 +32,21 @@ def tile_mix_lorab_sgd_kernel(tc, x, dn, hs_words, hs_scales, dy0, dy1, prm, out
     r_tiles = R // P
 
     with ExitStack() as ctx:
-        raw = ctx.enter_context(tc.tile_pool(name="raw", bufs=4))
+        raw = ctx.enter_context(tc.tile_pool(name="raw", bufs=1))
         keep = ctx.enter_context(tc.tile_pool(name="keep", bufs=1))
         stage = ctx.enter_context(tc.tile_pool(name="stage", bufs=6))
         psum = ctx.enter_context(tc.psum_pool(name="psum", bufs=1))
         ctx.enter_context(tc.manual_schedule())
 
-        def load_pass(src, a, name):
+        def load_passes(src, name, tag):
             width = src.shape[1]
-            t = raw.tile([P, PACK, width], F32, name=name, tag="raw")
-            nc.sync.dma_start(out=t[:], in_=src[a * PASS : (a + 1) * PASS, :].rearrange("(p j) w -> p j w", j=PACK))
-            return t
+            passes = src.shape[0] // PASS
+            t = raw.tile([P, passes, PACK, width], F32, name=name, tag=tag)
+            nc.sync.dma_start(
+                out=t[:].rearrange("p a j w -> p a (j w)"),
+                in_=src.rearrange("(a p j) w -> p a (j w)", a=passes, j=PACK),
+            )
+            return [t[:, a, :, :] for a in range(passes)]
 
         def planes(name, width):
             codes = keep.tile([P, width], U32, name=name + "_codes", align_bytes=64)
@@ -73,31 +77,27 @@ def tile_mix_lorab_sgd_kernel(tc, x, dn, hs_words, hs_scales, dy0, dy1, prm, out
             return psum.tile([P, BLK], F32, name=name, tag="bank%d" % i)
 
         hs_sc = keep.tile([P, 2, R], U8, name="hs_sc", align_bytes=64)
-        nc.gpsimd.memset(hs_sc[:].bitcast(U32), 0)
+        nc.vector.memset(hs_sc[:].bitcast(U32), 0)
         for q in range(4):
-            nc.gpsimd.dma_start(
+            nc.scalar.dma_start(
                 out=hs_sc[32 * q : 32 * q + 4, :, :].bitcast(I32),
                 in_=hs_scales[:, 4 * q : 4 * q + 4, :].rearrange("a r n -> r a n").bitcast(I32),
             )
 
-        x_raw = [load_pass(x, 0, "x_raw0")]
-        dn_raw = keep.tile([P, 2, PACK, R], F32, name="dn_raw")
-        nc.sync.dma_start(
-            out=dn_raw[:].rearrange("p a j r -> p a (j r)"), in_=dn.rearrange("(a p j) r -> p a (j r)", a=2, j=PACK)
-        )
-        x_raw.append(load_pass(x, 1, "x_raw1"))
+        dn_raw = load_passes(dn, "dn_raw", "slot_b")
+        x_raw = load_passes(x, "x_raw", "slot_a")
         hs_w = keep.tile([P, 2, 2 * R], U8, name="hs_w", align_bytes=64)
         nc.sync.dma_start(out=hs_w[:].bitcast(I32), in_=hs_words.rearrange("a p w -> p a w").bitcast(I32))
-        dy_raw = [load_pass(dy0, 0, "dy_raw0"), load_pass(dy0, 1, "dy_raw1")]
+        dy_raw = load_passes(dy0[:PASS, :], "dy0_raw0", "slot_c") + load_passes(dy0[PASS:, :], "dy0_raw1", "slot_e")
 
         x_q = [planes("x%d" % a, T) for a in range(2)]
         dn_q = [planes("dn%d" % a, R) for a in range(2)]
         h_q = [planes("h%d" % b, R) for b in range(2)]
         dy_q = [planes("dy%d" % g, N) for g in range(4)]
 
-        def x_pass(a):
+        def x_block(b):
             gs = []
-            for b, engine in enumerate(("vector", "scalar")):
+            for a, engine in enumerate(("vector", "scalar")):
                 g = staged("x_g%d%d" % (a, b))
                 copy_on(
                     engine,
@@ -105,30 +105,36 @@ def tile_mix_lorab_sgd_kernel(tc, x, dn, hs_words, hs_scales, dy0, dy1, prm, out
                     x_raw[a][:, :, b * BLK : (b + 1) * BLK].rearrange("p j (m t) -> p m j t", t=4),
                 )
                 gs.append(g)
-            for b in range(2):
-                quantize(gs[b], x_q[a], b * BLK, E4M3)
+            for a in range(2):
+                quantize(gs[a], x_q[a], b * BLK, E4M3)
 
-        x_pass(0)
         dn_g = []
         for a, engine in enumerate(("vector", "scalar")):
             g = staged("dn_g%d" % a)
-            interleave(engine, g[:], dn_raw[:, a, :, :])
+            interleave(engine, g[:], dn_raw[a])
             dn_g.append(g)
         for a in range(2):
             quantize(dn_g[a], dn_q[a], 0, E4M3)
-        x_pass(1)
+        x_block(0)
+        x_block(1)
 
-        dy_raw.append(load_pass(dy1, 0, "dy_raw2"))
+        dy_raw.extend(load_passes(dy1[:PASS, :], "dy1_raw", "slot_a"))
         last_rows = dy1[PASS:, :].rearrange("(p j) w -> p j w", j=PACK)
         halves = []
 
         def load_half(u):
             c0, c1 = ((0, 2 * BLK), (2 * BLK, N))[u]
-            t = raw.tile([P, PACK, c1 - c0], F32, name="dy_half%d" % u, tag="raw")
+            t = raw.tile([P, PACK, c1 - c0], F32, name="dy_half%d" % u, tag=("slot_b", "slot_d")[u])
             nc.sync.dma_start(out=t[:], in_=last_rows[:, :, c0:c1])
             halves.append(t)
 
         load_half(0)
+        load_half(1)
+        prm_t = []
+        for u in range(2):
+            t = keep.tile([P, 2, N], F32, name="prm%d" % u)
+            nc.sync.dma_start(out=t[:], in_=prm[2 * u * P : 2 * (u + 1) * P, :].rearrange("(i p) n -> p i n", i=2))
+            prm_t.extend([t[:, 0, :], t[:, 1, :]])
 
         def h_products(b):
             banks = []
@@ -198,12 +204,6 @@ def tile_mix_lorab_sgd_kernel(tc, x, dn, hs_words, hs_scales, dy0, dy1, prm, out
         for rt in range(r_tiles):
             acc[rt, 0] = bank_tile(rt, "acc%d0" % rt)
         dy_pass(0, {0: [(0, 0)]})
-        load_half(1)
-        prm_t = []
-        for rt in range(r_tiles):
-            t = keep.tile([P, N], F32, name="prm%d" % rt)
-            nc.sync.dma_start(out=t[:], in_=prm[rt * P : (rt + 1) * P, :])
-            prm_t.append(t)
         h_quantize(1, h_banks[1], "scalar")
         for rt in range(r_tiles):
             acc[rt, 1] = bank_tile(r_tiles + rt, "acc%d1" % rt)
@@ -240,4 +240,4 @@ def tile_mix_lorab_sgd_kernel(tc, x, dn, hs_words, hs_scales, dy0, dy1, prm, out
                 nc.vector.scalar_tensor_tensor(
                     out=prm_t[rt][:, cols], in0=acc[rt, nb][:], scalar=STEP, in1=prm_t[rt][:, cols], op0=ALU.mult, op1=ALU.add
                 )
-            nc.sync.dma_start(out=out[rt * P : (rt + 1) * P, :], in_=prm_t[rt][:])
+            nc.sync.dma_start(out=out[rt * P : (rt + 1) * P, :], in_=prm_t[rt])

@@ -78,13 +78,12 @@ def tile_mix_lorab_sgd_kernel(tc, x, dn, hs_words, hs_scales, dy0, dy1, prm, out
 
         hs_sc = keep.tile([P, 2, R], U8, name="hs_sc", align_bytes=64)
         nc.vector.memset(hs_sc[:].bitcast(U32), 0)
-        for q in range(4):
-            nc.scalar.dma_start(
-                out=hs_sc[32 * q : 32 * q + 4, :, :].bitcast(I32),
-                in_=hs_scales[:, 4 * q : 4 * q + 4, :].rearrange("a r n -> r a n").bitcast(I32),
-            )
-
         dn_raw = load_passes(dn, "dn_raw", "slot_b")
+        for r in range(4):
+            nc.sync.dma_start(
+                out=hs_sc[r:P:32, :, :].bitcast(I32),
+                in_=hs_scales[:, r:16:4, :].rearrange("a q n -> q a n").bitcast(I32),
+            )
         x_raw = load_passes(x, "x_raw", "slot_a")
         hs_w = keep.tile([P, 2, 2 * R], U8, name="hs_w", align_bytes=64)
         nc.sync.dma_start(out=hs_w[:].bitcast(I32), in_=hs_words.rearrange("a p w -> p a w").bitcast(I32))

@@ -21,7 +21,7 @@ PACK = 4
 PASS = P * PACK
 BLK = 512
 BANKS = 8
-V_COLS = 288
+V_COLS = 256
 V_COLS_PAIR = 256
 V_COLS_LAST = 384
 
@@ -87,7 +87,7 @@ def tile_mix_lorab_sgd_kernel(tc, x, dn, hs_words, hs_scales, dy0, dy1, prm, out
         x_raw = load_passes(x, "x_raw", "slot_a")
         hs_w = keep.tile([P, 2, 2 * R], U8, name="hs_w", align_bytes=64)
         nc.sync.dma_start(out=hs_w[:].bitcast(I32), in_=hs_words.rearrange("a p w -> p a w").bitcast(I32))
-        dy_raw = load_passes(dy0[:PASS, :], "dy0_raw0", "slot_c") + load_passes(dy0[PASS:, :], "dy0_raw1", "slot_e")
+        dy_raw = load_passes(dy0, "dy0_raw", "slot_c")
 
         x_q = [planes("x%d" % a, T) for a in range(2)]
         dn_q = [planes("dn%d" % a, R) for a in range(2)]
@@ -162,6 +162,7 @@ def tile_mix_lorab_sgd_kernel(tc, x, dn, hs_words, hs_scales, dy0, dy1, prm, out
 
         h_banks = [h_products(b) for b in range(2)]
         h_quantize(0, h_banks[0], "vector")
+        h_quantize(1, h_banks[1], "scalar")
 
         acc = {}
 
@@ -203,7 +204,6 @@ def tile_mix_lorab_sgd_kernel(tc, x, dn, hs_words, hs_scales, dy0, dy1, prm, out
         for rt in range(r_tiles):
             acc[rt, 0] = bank_tile(rt, "acc%d0" % rt)
         dy_pass(0, {0: [(0, 0)]})
-        h_quantize(1, h_banks[1], "scalar")
         for rt in range(r_tiles):
             acc[rt, 1] = bank_tile(r_tiles + rt, "acc%d1" % rt)
         db_column(1, 0)

@@ -41,7 +41,7 @@ def tile_mix_lorab_sgd_kernel(tc, x, dn, hs_words, hs_scales, dy0, dy1, prm, out
         def load_passes(src, name, tag):
             width = src.shape[1]
             passes = src.shape[0] // PASS
-            t = raw.tile([P, passes, PACK, width], F32, name=name, tag=tag)
+            t = raw.tile([P, passes, PACK, width], F32, name=name, tag=tag, align_bytes=256)
             nc.sync.dma_start(
                 out=t[:].rearrange("p a j w -> p a (j w)"),
                 in_=src.rearrange("(a p j) w -> p a (j w)", a=passes, j=PACK),
@@ -76,7 +76,7 @@ def tile_mix_lorab_sgd_kernel(tc, x, dn, hs_words, hs_scales, dy0, dy1, prm, out
         def bank_tile(i, name):
             return psum.tile([P, BLK], F32, name=name, tag="bank%d" % i)
 
-        hs_sc = keep.tile([P, 2, R], U8, name="hs_sc", align_bytes=64)
+        hs_sc = keep.tile([P, 2, R], U8, name="hs_sc", align_bytes=256)
         nc.vector.memset(hs_sc[:].bitcast(U32), 0)
         dn_raw = load_passes(dn, "dn_raw", "slot_b")
         for r in range(4):
@@ -85,7 +85,7 @@ def tile_mix_lorab_sgd_kernel(tc, x, dn, hs_words, hs_scales, dy0, dy1, prm, out
                 in_=hs_scales[:, r:16:4, :].rearrange("a q n -> q a n").bitcast(I32),
             )
         x_raw = load_passes(x, "x_raw", "slot_a")
-        hs_w = keep.tile([P, 2, 2 * R], U8, name="hs_w", align_bytes=64)
+        hs_w = keep.tile([P, 2, 2 * R], U8, name="hs_w", align_bytes=256)
         nc.sync.dma_start(out=hs_w[:].bitcast(I32), in_=hs_words.rearrange("a p w -> p a w").bitcast(I32))
         dy_raw = load_passes(dy0, "dy0_raw", "slot_c")
 
@@ -123,7 +123,7 @@ def tile_mix_lorab_sgd_kernel(tc, x, dn, hs_words, hs_scales, dy0, dy1, prm, out
 
         def load_half(u):
             c0, c1 = ((0, 2 * BLK), (2 * BLK, N))[u]
-            t = raw.tile([P, PACK, c1 - c0], F32, name="dy_half%d" % u, tag=("slot_b", "slot_d")[u])
+            t = raw.tile([P, PACK, c1 - c0], F32, name="dy_half%d" % u, tag=("slot_b", "slot_d")[u], align_bytes=256)
             nc.sync.dma_start(out=t[:], in_=last_rows[:, :, c0:c1])
             halves.append(t)
 
@@ -131,7 +131,7 @@ def tile_mix_lorab_sgd_kernel(tc, x, dn, hs_words, hs_scales, dy0, dy1, prm, out
         load_half(1)
         prm_t = []
         for u in range(2):
-            t = keep.tile([P, 2, N], F32, name="prm%d" % u)
+            t = keep.tile([P, 2, N], F32, name="prm%d" % u, align_bytes=256)
             nc.sync.dma_start(out=t[:], in_=prm[2 * u * P : 2 * (u + 1) * P, :].rearrange("(i p) n -> p i n", i=2))
             prm_t.extend([t[:, 0, :], t[:, 1, :]])
 

@@ -87,7 +87,7 @@ def tile_mix_lorab_sgd_kernel(tc, x, dn, hs_words, hs_scales, dy0, dy1, prm, out
         x_raw = load_passes(x, "x_raw", "slot_a")
         hs_w = keep.tile([P, 2, 2 * R], U8, name="hs_w", align_bytes=256)
         nc.sync.dma_start(out=hs_w[:].bitcast(I32), in_=hs_words.rearrange("a p w -> p a w").bitcast(I32))
-        dy_raw = load_passes(dy0, "dy0_raw", "slot_c")
+        dy_raw = load_passes(dy0[:PASS, :], "dy0_raw0", "slot_c") + load_passes(dy0[PASS:, :], "dy0_raw1", "slot_e")
 
         x_q = [planes("x%d" % a, T) for a in range(2)]
         dn_q = [planes("dn%d" % a, R) for a in range(2)]

@@ -130,10 +130,10 @@ def tile_mix_lorab_sgd_kernel(tc, x, dn, hs_words, hs_scales, dy0, dy1, prm, out
         load_half(0)
         load_half(1)
         prm_t = []
-        for u in range(2):
-            t = keep.tile([P, 2, N], F32, name="prm%d" % u, align_bytes=256)
-            nc.sync.dma_start(out=t[:], in_=prm[2 * u * P : 2 * (u + 1) * P, :].rearrange("(i p) n -> p i n", i=2))
-            prm_t.extend([t[:, 0, :], t[:, 1, :]])
+        for rt in range(r_tiles):
+            t = keep.tile([P, N], F32, name="prm%d" % rt, align_bytes=256)
+            nc.sync.dma_start(out=t[:], in_=prm[rt * P : (rt + 1) * P, :])
+            prm_t.append(t[:])
 
         def h_products(b):
             banks = []

@@ -22,8 +22,7 @@ PASS = P * PACK
 BLK = 512
 BANKS = 8
 V_COLS = 256
-V_COLS_PAIR = 256
-V_COLS_LAST = 384
+V_COLS_LAST = 304
 
 
 def tile_mix_lorab_sgd_kernel(tc, x, dn, hs_words, hs_scales, dy0, dy1, prm, out):
@@ -85,9 +84,13 @@ def tile_mix_lorab_sgd_kernel(tc, x, dn, hs_words, hs_scales, dy0, dy1, prm, out
                 in_=hs_scales[:, r:16:4, :].rearrange("a q n -> q a n").bitcast(I32),
             )
         x_raw = load_passes(x, "x_raw", "slot_a")
-        hs_w = keep.tile([P, 2, 2 * R], U8, name="hs_w", align_bytes=256)
-        nc.sync.dma_start(out=hs_w[:].bitcast(I32), in_=hs_words.rearrange("a p w -> p a w").bitcast(I32))
-        dy_raw = load_passes(dy0[:PASS, :], "dy0_raw0", "slot_c") + load_passes(dy0[PASS:, :], "dy0_raw1", "slot_e")
+        hs_w = [keep.tile([P, 2 * R], U8, name="hs_w%d" % a, align_bytes=256) for a in range(2)]
+
+        def load_hs(a):
+            nc.sync.dma_start(out=hs_w[a][:].bitcast(I32), in_=hs_words[a].bitcast(I32))
+
+        load_hs(0)
+        dy_raw = load_passes(dy1[:PASS, :], "dy1_raw0", "slot_c") + load_passes(dy1[PASS:, :], "dy1_raw1", "slot_e")
 
         x_q = [planes("x%d" % a, T) for a in range(2)]
         dn_q = [planes("dn%d" % a, R) for a in range(2)]
@@ -117,18 +120,9 @@ def tile_mix_lorab_sgd_kernel(tc, x, dn, hs_words, hs_scales, dy0, dy1, prm, out
         x_block(0)
         x_block(1)
 
-        dy_raw.extend(load_passes(dy1[:PASS, :], "dy1_raw", "slot_a"))
-        last_rows = dy1[PASS:, :].rearrange("(p j) w -> p j w", j=PACK)
-        halves = []
-
-        def load_half(u):
-            c0, c1 = ((0, 2 * BLK), (2 * BLK, N))[u]
-            t = raw.tile([P, PACK, c1 - c0], F32, name="dy_half%d" % u, tag=("slot_b", "slot_d")[u], align_bytes=256)
-            nc.sync.dma_start(out=t[:], in_=last_rows[:, :, c0:c1])
-            halves.append(t)
-
-        load_half(0)
-        load_half(1)
+        dy_raw.extend(load_passes(dy0[:PASS, :], "dy0_raw0", "slot_a"))
+        dy_raw.extend(load_passes(dy0[PASS:, :], "dy0_raw1", "slot_b"))
+        load_hs(1)
         prm_t = []
         for rt in range(r_tiles):
             t = keep.tile([P, N], F32, name="prm%d" % rt, align_bytes=256)
@@ -168,11 +162,11 @@ def tile_mix_lorab_sgd_kernel(tc, x, dn, hs_words, hs_scales, dy0, dy1, prm, out
 
         def db_pass(rt, nb, g):
             if g < 2:
-                lhsT = hs_w[:, g, 2 * P * rt : 2 * P * (rt + 1)].bitcast(E2M1)
-                lhsT_scale = hs_sc[:, g, P * rt : P * (rt + 1)]
+                lhsT = h_q[g][0][:, P * rt : P * (rt + 1)].bitcast(E4M3)
+                lhsT_scale = h_q[g][1][:, P * rt : P * (rt + 1)]
             else:
-                lhsT = h_q[g - 2][0][:, P * rt : P * (rt + 1)].bitcast(E4M3)
-                lhsT_scale = h_q[g - 2][1][:, P * rt : P * (rt + 1)]
+                lhsT = hs_w[g - 2][:, 2 * P * rt : 2 * P * (rt + 1)].bitcast(E2M1)
+                lhsT_scale = hs_sc[:, g - 2, P * rt : P * (rt + 1)]
             nc.tensor.matmul_mx(
                 out=acc[rt, nb][:],
                 lhsT=lhsT,
@@ -183,60 +177,55 @@ def tile_mix_lorab_sgd_kernel(tc, x, dn, hs_words, hs_scales, dy0, dy1, prm, out
                 stop=(g == 3),
             )
 
-        def db_column(nb, g):
-            for rt in range(r_tiles):
-                db_pass(rt, nb, g)
-
         def copy_block(g_tile, src, c0, v_cols):
             interleave("vector", g_tile[:, :v_cols, :], src[:, :, c0 : c0 + v_cols])
             interleave("scalar", g_tile[:, v_cols:, :], src[:, :, c0 + v_cols : c0 + BLK])
 
-        def dy_pass(g, after_block):
+        def dy_pass(g, v_cols, after_block):
             gs = [staged("dy_g%d%d" % (g, nb)) for nb in range(n_blocks)]
             for nb in range(n_blocks + 1):
                 if nb < n_blocks:
-                    copy_block(gs[nb], dy_raw[g], nb * BLK, V_COLS)
+                    copy_block(gs[nb], dy_raw[g], nb * BLK, v_cols)
                 if nb > 0:
                     quantize(gs[nb - 1], dy_q[g], (nb - 1) * BLK, E5M2)
-                    for key in after_block.get(nb - 1, []):
-                        db_column(*key)
+                    for rt, col in after_block[nb - 1]:
+                        db_pass(rt, col, g)
 
-        for rt in range(r_tiles):
-            acc[rt, 0] = bank_tile(rt, "acc%d0" % rt)
-        dy_pass(0, {0: [(0, 0)]})
-        for rt in range(r_tiles):
-            acc[rt, 1] = bank_tile(r_tiles + rt, "acc%d1" % rt)
-        db_column(1, 0)
-        dy_pass(1, {1: [(1, 1)]})
-        dy_pass(2, {0: [(0, 1), (0, 2)], 1: [(1, 2)]})
-
-        gs = [staged("dy_g3%d" % nb) for nb in range(n_blocks)]
-        for nb in range(2):
-            copy_block(gs[nb], halves[0], nb * BLK, V_COLS_PAIR)
-        leave_order = [1, 2, 0, 3]
-        quantize(gs[0], dy_q[3], 0, E5M2)
-        for rt in leave_order:
-            db_pass(rt, 0, 3)
-        quantize(gs[1], dy_q[3], BLK, E5M2)
-        copy_block(gs[2], halves[1], 0, V_COLS_LAST)
-        quantize(gs[2], dy_q[3], 2 * BLK, E5M2)
+        tiles = [(rt, nb) for rt in range(r_tiles) for nb in range(n_blocks)]
+        resident = sorted(tiles[:BANKS], key=lambda t: t[1])
+        late = tiles[BANKS:]
+        bank_of = {}
+        for i, key in enumerate(resident):
+            bank_of[key] = i
+            acc[key] = bank_tile(i, "acc%d%d" % key)
+        for g in range(2):
+            dy_pass(g, V_COLS, [[t for t in resident if t[1] == nb] for nb in range(n_blocks)])
+        dy_pass(2, V_COLS, [[], [], sorted(resident, key=lambda t: -t[1])])
+        dy_pass(3, V_COLS_LAST, [[(0, 0), (1, 0), (2, 0)], [(0, 1), (1, 1)], [(0, 2), (1, 2), (2, 1)]])
 
         part = {}
-        for rt, left in enumerate(leave_order):
-            part[left] = keep.tile([P, BLK], F32, name="part%d" % left)
-            nc.scalar.mul(out=part[left][:], in_=acc[left, 0][:], mul=STEP)
-            acc[rt, 2] = bank_tile(left, "acc%d2" % rt)
+        for rt in range(3):
+            part[rt] = keep.tile([P, BLK], F32, name="part%d" % rt)
+            nc.scalar.mul(out=part[rt][:], in_=acc[rt, 0][:], mul=STEP)
 
-        for rt in range(r_tiles):
-            db_pass(rt, 1, 3)
-            for g in range(4):
-                db_pass(rt, 2, g)
-
-        for rt in range(r_tiles):
-            nc.gpsimd.tensor_tensor(out=prm_t[rt][:, :BLK], in0=part[rt][:], in1=prm_t[rt][:, :BLK], op=ALU.add)
-            for nb in range(1, n_blocks):
-                cols = slice(nb * BLK, (nb + 1) * BLK)
+        def finish(rt, nb):
+            cols = slice(nb * BLK, (nb + 1) * BLK)
+            if nb == 0 and rt in part:
+                nc.gpsimd.tensor_tensor(out=prm_t[rt][:, cols], in0=part[rt][:], in1=prm_t[rt][:, cols], op=ALU.add)
+            else:
                 nc.vector.scalar_tensor_tensor(
                     out=prm_t[rt][:, cols], in0=acc[rt, nb][:], scalar=STEP, in1=prm_t[rt][:, cols], op0=ALU.mult, op1=ALU.add
                 )
+
+        def row_tile_out(rt):
+            for nb in range(n_blocks):
+                finish(rt, nb)
             nc.sync.dma_start(out=out[rt * P : (rt + 1) * P, :], in_=prm_t[rt])
+
+        row_tile_out(0)
+        for key, left in zip(late, [(0, 0), (1, 0), (0, 1), (2, 0)]):
+            acc[key] = bank_tile(bank_of[left], "acc%d%d" % key)
+            for g in range(4):
+                db_pass(key[0], key[1], g)
+        for rt in range(1, r_tiles):
+            row_tile_out(rt)

@@ -22,7 +22,8 @@ PASS = P * PACK
 BLK = 512
 BANKS = 8
 V_COLS = 256
-V_COLS_LAST = 304
+V_COLS_FIRST = 336
+V_COLS_LAST = 256
 
 
 def tile_mix_lorab_sgd_kernel(tc, x, dn, hs_words, hs_scales, dy0, dy1, prm, out):
@@ -121,7 +122,12 @@ def tile_mix_lorab_sgd_kernel(tc, x, dn, hs_words, hs_scales, dy0, dy1, prm, out
         x_block(1)
 
         dy_raw.extend(load_passes(dy0[:PASS, :], "dy0_raw0", "slot_a"))
-        dy_raw.extend(load_passes(dy0[PASS:, :], "dy0_raw1", "slot_b"))
+        last = raw.tile([P, PACK * N], F32, name="dy0_raw1", tag="slot_b", align_bytes=256)
+        last_rows = dy0[PASS:, :].rearrange("(p j) w -> p (j w)", j=PACK)
+        cut = (PACK - 1) * N + BLK
+        nc.sync.dma_start(out=last[:, :cut], in_=last_rows[:, :cut])
+        nc.sync.dma_start(out=last[:, cut:], in_=last_rows[:, cut:])
+        dy_raw.append(last[:].rearrange("p (j w) -> p j w", j=PACK))
         load_hs(1)
         prm_t = []
         for rt in range(r_tiles):
@@ -192,8 +198,8 @@ def tile_mix_lorab_sgd_kernel(tc, x, dn, hs_words, hs_scales, dy0, dy1, prm, out
                         db_pass(rt, col, g)
 
         tiles = [(rt, nb) for rt in range(r_tiles) for nb in range(n_blocks)]
-        resident = sorted(tiles[:BANKS], key=lambda t: t[1])
-        late = tiles[BANKS:]
+        late = [(rt, nb) for rt, nb in tiles if rt >= 2 and nb >= 1]
+        resident = sorted([t for t in tiles if t not in late], key=lambda t: t[1])
         bank_of = {}
         for i, key in enumerate(resident):
             bank_of[key] = i
@@ -201,16 +207,29 @@ def tile_mix_lorab_sgd_kernel(tc, x, dn, hs_words, hs_scales, dy0, dy1, prm, out
         for g in range(2):
             dy_pass(g, V_COLS, [[t for t in resident if t[1] == nb] for nb in range(n_blocks)])
         dy_pass(2, V_COLS, [[], [], sorted(resident, key=lambda t: -t[1])])
-        dy_pass(3, V_COLS_LAST, [[(0, 0), (1, 0), (2, 0)], [(0, 1), (1, 1)], [(0, 2), (1, 2), (2, 1)]])
+        gs = [staged("dy_g3%d" % nb) for nb in range(n_blocks)]
+
+        def close_block(nb):
+            quantize(gs[nb], dy_q[3], nb * BLK, E5M2)
+            for rt, col in resident:
+                if col == nb:
+                    db_pass(rt, col, 3)
+
+        copy_block(gs[0], dy_raw[3], 0, V_COLS_FIRST)
+        close_block(0)
+        copy_block(gs[1], dy_raw[3], BLK, V_COLS_LAST)
+        copy_block(gs[2], dy_raw[3], 2 * BLK, V_COLS_LAST)
+        close_block(1)
+        close_block(2)
 
         part = {}
-        for rt in range(3):
+        for rt in range(r_tiles):
             part[rt] = keep.tile([P, BLK], F32, name="part%d" % rt)
             nc.scalar.mul(out=part[rt][:], in_=acc[rt, 0][:], mul=STEP)
 
         def finish(rt, nb):
             cols = slice(nb * BLK, (nb + 1) * BLK)
-            if nb == 0 and rt in part:
+            if nb == 0:
                 nc.gpsimd.tensor_tensor(out=prm_t[rt][:, cols], in0=part[rt][:], in1=prm_t[rt][:, cols], op=ALU.add)
             else:
                 nc.vector.scalar_tensor_tensor(
@@ -223,7 +242,7 @@ def tile_mix_lorab_sgd_kernel(tc, x, dn, hs_words, hs_scales, dy0, dy1, prm, out
             nc.sync.dma_start(out=out[rt * P : (rt + 1) * P, :], in_=prm_t[rt])
 
         row_tile_out(0)
-        for key, left in zip(late, [(0, 0), (1, 0), (0, 1), (2, 0)]):
+        for key, left in zip(late, [(rt, 0) for rt in range(r_tiles)]):
             acc[key] = bank_tile(bank_of[left], "acc%d%d" % key)
             for g in range(4):
                 db_pass(key[0], key[1], g)

@@ -38,11 +38,11 @@ def tile_mix_lorab_sgd_kernel(tc, x, dn, hs_words, hs_scales, dy0, dy1, prm, out
         psum = ctx.enter_context(tc.psum_pool(name="psum", bufs=1))
         ctx.enter_context(tc.manual_schedule())
 
-        def load_passes(src, name, tag):
+        def load_passes(src, name, tag, queue=nc.sync):
             width = src.shape[1]
             passes = src.shape[0] // PASS
             t = raw.tile([P, passes, PACK, width], F32, name=name, tag=tag, align_bytes=256)
-            nc.sync.dma_start(
+            queue.dma_start(
                 out=t[:].rearrange("p a j w -> p a (j w)"),
                 in_=src.rearrange("(a p j) w -> p a (j w)", a=passes, j=PACK),
             )
@@ -78,9 +78,9 @@ def tile_mix_lorab_sgd_kernel(tc, x, dn, hs_words, hs_scales, dy0, dy1, prm, out
 
         hs_sc = keep.tile([P, 2, R], U8, name="hs_sc", align_bytes=256)
         nc.vector.memset(hs_sc[:].bitcast(U32), 0)
-        dn_raw = load_passes(dn, "dn_raw", "slot_b")
+        dn_raw = load_passes(dn, "dn_raw", "slot_b", nc.scalar)
         for r in range(4):
-            nc.sync.dma_start(
+            nc.scalar.dma_start(
                 out=hs_sc[r:P:32, :, :].bitcast(I32),
                 in_=hs_scales[:, r:16:4, :].rearrange("a q n -> q a n").bitcast(I32),
             )
@@ -239,7 +239,7 @@ def tile_mix_lorab_sgd_kernel(tc, x, dn, hs_words, hs_scales, dy0, dy1, prm, out
         def row_tile_out(rt):
             for nb in range(n_blocks):
                 finish(rt, nb)
-            nc.sync.dma_start(out=out[rt * P : (rt + 1) * P, :], in_=prm_t[rt])
+            (nc.sync, nc.scalar)[rt % 2].dma_start(out=out[rt * P : (rt + 1) * P, :], in_=prm_t[rt])
 
         row_tile_out(0)
         for key, left in zip(late, [(rt, 0) for rt in range(r_tiles)]):

@@ -78,13 +78,13 @@ def tile_mix_lorab_sgd_kernel(tc, x, dn, hs_words, hs_scales, dy0, dy1, prm, out
 
         hs_sc = keep.tile([P, 2, R], U8, name="hs_sc", align_bytes=256)
         nc.vector.memset(hs_sc[:].bitcast(U32), 0)
-        dn_raw = load_passes(dn, "dn_raw", "slot_b", nc.scalar)
+        dn_raw = load_passes(dn[:PASS, :], "dn_raw0", "slot_b", nc.scalar) + load_passes(dn[PASS:, :], "dn_raw1", "slot_f", nc.scalar)
         for r in range(4):
             nc.scalar.dma_start(
                 out=hs_sc[r:P:32, :, :].bitcast(I32),
                 in_=hs_scales[:, r:16:4, :].rearrange("a q n -> q a n").bitcast(I32),
             )
-        x_raw = load_passes(x, "x_raw", "slot_a")
+        x_raw = load_passes(x[:PASS, :], "x_raw0", "slot_a") + load_passes(x[PASS:, :], "x_raw1", "slot_g")
         hs_w = [keep.tile([P, 2 * R], U8, name="hs_w%d" % a, align_bytes=256) for a in range(2)]
 
         def load_hs(a):

@@ -77,7 +77,6 @@ def tile_mix_lorab_sgd_kernel(tc, x, dn, hs_words, hs_scales, dy0, dy1, prm, out
             return psum.tile([P, BLK], F32, name=name, tag="bank%d" % i)
 
         hs_sc = keep.tile([P, 2, R], U8, name="hs_sc", align_bytes=256)
-        nc.vector.memset(hs_sc[:].bitcast(U32), 0)
         dn_raw = load_passes(dn[:PASS, :], "dn_raw0", "slot_b", nc.scalar) + load_passes(dn[PASS:, :], "dn_raw1", "slot_f", nc.scalar)
         for r in range(4):
             nc.scalar.dma_start(

@@ -20,16 +20,14 @@ P = 128
 PACK = 4
 PASS = P * PACK
 BLK = 512
-BANKS = 8
+N_BLOCKS = N // BLK
+R_TILES = R // P
 V_COLS = 256
-V_COLS_FIRST = 336
-V_COLS_LAST = 256
+V_COLS_LAST = (336, 256, 256)
 
 
 def tile_mix_lorab_sgd_kernel(tc, x, dn, hs_words, hs_scales, dy0, dy1, prm, out):
     nc = tc.nc
-    n_blocks = N // BLK
-    r_tiles = R // P
 
     with ExitStack() as ctx:
         raw = ctx.enter_context(tc.tile_pool(name="raw", bufs=1))
@@ -38,15 +36,11 @@ def tile_mix_lorab_sgd_kernel(tc, x, dn, hs_words, hs_scales, dy0, dy1, prm, out
         psum = ctx.enter_context(tc.psum_pool(name="psum", bufs=1))
         ctx.enter_context(tc.manual_schedule())
 
-        def load_passes(src, name, tag, queue=nc.sync):
+        def load_pass(queue, src, a, name, slot):
             width = src.shape[1]
-            passes = src.shape[0] // PASS
-            t = raw.tile([P, passes, PACK, width], F32, name=name, tag=tag, align_bytes=256)
-            queue.dma_start(
-                out=t[:].rearrange("p a j w -> p a (j w)"),
-                in_=src.rearrange("(a p j) w -> p a (j w)", a=passes, j=PACK),
-            )
-            return [t[:, a, :, :] for a in range(passes)]
+            t = raw.tile([P, PACK * width], F32, name=name, tag=slot, align_bytes=256)
+            queue.dma_start(out=t[:], in_=src[a * PASS : (a + 1) * PASS, :].rearrange("(p j) w -> p (j w)", j=PACK))
+            return t[:].rearrange("p (j w) -> p j w", j=PACK)
 
         def planes(name, width):
             codes = keep.tile([P, width], U32, name=name + "_codes", align_bytes=64)
@@ -56,14 +50,14 @@ def tile_mix_lorab_sgd_kernel(tc, x, dn, hs_words, hs_scales, dy0, dy1, prm, out
         def staged(name):
             return stage.tile([P, BLK, PACK], BF16, name=name, tag="stage", align_bytes=64)
 
-        def copy_on(engine, dst, src):
-            if engine == "vector":
-                nc.vector.tensor_copy(out=dst, in_=src)
-            else:
-                nc.scalar.copy(out=dst, in_=src)
+        def vector_copy(dst, src):
+            nc.vector.tensor_copy(out=dst, in_=src)
 
-        def interleave(engine, dst, src):
-            copy_on(engine, dst.rearrange("p (c i) j -> p c j i", i=4), src.rearrange("p j (c i) -> p c j i", i=4))
+        def scalar_copy(dst, src):
+            nc.scalar.copy(out=dst, in_=src)
+
+        def interleave(copy, dst, src):
+            copy(dst.rearrange("p (c i) j -> p c j i", i=4), src.rearrange("p j (c i) -> p c j i", i=4))
 
         def quantize(g, plane, col0, fmt):
             codes, scales = plane
@@ -77,50 +71,44 @@ def tile_mix_lorab_sgd_kernel(tc, x, dn, hs_words, hs_scales, dy0, dy1, prm, out
             return psum.tile([P, BLK], F32, name=name, tag="bank%d" % i)
 
         hs_sc = keep.tile([P, 2, R], U8, name="hs_sc", align_bytes=256)
-        dn_raw = load_passes(dn[:PASS, :], "dn_raw0", "slot_b", nc.scalar) + load_passes(dn[PASS:, :], "dn_raw1", "slot_f", nc.scalar)
+        hs_w = [keep.tile([P, 2 * R], U8, name="hs_w%d" % a, align_bytes=256) for a in range(2)]
+        prm_t = [keep.tile([P, N], F32, name="prm%d" % rt, align_bytes=256) for rt in range(R_TILES)]
+
+        def load_hs(a):
+            nc.sync.dma_start(out=hs_w[a][:].bitcast(I32), in_=hs_words[a].bitcast(I32))
+
+        dn_raw = [load_pass(nc.scalar, dn, a, "dn_raw%d" % a, slot) for a, slot in enumerate(("slot_b", "slot_f"))]
+        x_raw = [load_pass(nc.sync, x, a, "x_raw%d" % a, slot) for a, slot in enumerate(("slot_a", "slot_g"))]
         for r in range(4):
             nc.scalar.dma_start(
                 out=hs_sc[r:P:32, :, :].bitcast(I32),
                 in_=hs_scales[:, r:16:4, :].rearrange("a q n -> q a n").bitcast(I32),
             )
-        x_raw = load_passes(x[:PASS, :], "x_raw0", "slot_a") + load_passes(x[PASS:, :], "x_raw1", "slot_g")
-        hs_w = [keep.tile([P, 2 * R], U8, name="hs_w%d" % a, align_bytes=256) for a in range(2)]
-
-        def load_hs(a):
-            nc.sync.dma_start(out=hs_w[a][:].bitcast(I32), in_=hs_words[a].bitcast(I32))
-
         load_hs(0)
-        dy_raw = load_passes(dy1[:PASS, :], "dy1_raw0", "slot_c") + load_passes(dy1[PASS:, :], "dy1_raw1", "slot_e")
+        dy_raw = [load_pass(nc.sync, dy1, 0, "dy1_raw0", "slot_c"), load_pass(nc.scalar, dy1, 1, "dy1_raw1", "slot_e")]
 
         x_q = [planes("x%d" % a, T) for a in range(2)]
         dn_q = [planes("dn%d" % a, R) for a in range(2)]
         h_q = [planes("h%d" % b, R) for b in range(2)]
         dy_q = [planes("dy%d" % g, N) for g in range(4)]
+        copies = (vector_copy, scalar_copy)
 
-        def x_block(b):
-            gs = []
-            for a, engine in enumerate(("vector", "scalar")):
-                g = staged("x_g%d%d" % (a, b))
-                copy_on(
-                    engine,
-                    g[:].rearrange("p (t m) j -> p m j t", t=4),
-                    x_raw[a][:, :, b * BLK : (b + 1) * BLK].rearrange("p j (m t) -> p m j t", t=4),
-                )
-                gs.append(g)
-            for a in range(2):
-                quantize(gs[a], x_q[a], b * BLK, E4M3)
-
-        dn_g = []
-        for a, engine in enumerate(("vector", "scalar")):
-            g = staged("dn_g%d" % a)
-            interleave(engine, g[:], dn_raw[a])
-            dn_g.append(g)
+        dn_g = [staged("dn_g%d" % a) for a in range(2)]
+        for a in range(2):
+            interleave(copies[a], dn_g[a][:], dn_raw[a])
         for a in range(2):
             quantize(dn_g[a], dn_q[a], 0, E4M3)
-        x_block(0)
-        x_block(1)
+        for b in range(2):
+            x_g = [staged("x_g%d%d" % (a, b)) for a in range(2)]
+            for a in range(2):
+                copies[a](
+                    x_g[a][:].rearrange("p (t m) j -> p m j t", t=PACK),
+                    x_raw[a][:, :, b * BLK : (b + 1) * BLK].rearrange("p j (m t) -> p m j t", t=PACK),
+                )
+            for a in range(2):
+                quantize(x_g[a], x_q[a], b * BLK, E4M3)
 
-        dy_raw.extend(load_passes(dy0[:PASS, :], "dy0_raw0", "slot_a"))
+        dy_raw.append(load_pass(nc.sync, dy0, 0, "dy0_raw0", "slot_a"))
         last = raw.tile([P, PACK * N], F32, name="dy0_raw1", tag="slot_b", align_bytes=256)
         last_rows = dy0[PASS:, :].rearrange("(p j) w -> p (j w)", j=PACK)
         cut = (PACK - 1) * N + BLK
@@ -128,23 +116,20 @@ def tile_mix_lorab_sgd_kernel(tc, x, dn, hs_words, hs_scales, dy0, dy1, prm, out
         nc.sync.dma_start(out=last[:, cut:], in_=last_rows[:, cut:])
         dy_raw.append(last[:].rearrange("p (j w) -> p j w", j=PACK))
         load_hs(1)
-        prm_t = []
-        for rt in range(r_tiles):
-            t = keep.tile([P, N], F32, name="prm%d" % rt, align_bytes=256)
-            nc.sync.dma_start(out=t[:], in_=prm[rt * P : (rt + 1) * P, :])
-            prm_t.append(t[:])
+        for rt in range(R_TILES):
+            nc.sync.dma_start(out=prm_t[rt][:], in_=prm[rt * P : (rt + 1) * P, :])
 
         def h_products(b):
             banks = []
-            for rt in range(r_tiles):
-                bank = bank_tile(b * r_tiles + rt, "h_bank%d%d" % (b, rt))
+            for rt in range(R_TILES):
+                bank = bank_tile(b * R_TILES + rt, "h_bank%d%d" % (b, rt))
                 for j in range(PACK):
-                    tc0 = b * BLK + j * P
+                    t0 = b * BLK + j * P
                     for a in range(2):
                         nc.tensor.matmul_mx(
                             out=bank[:, j * P : (j + 1) * P],
-                            lhsT=x_q[a][0][:, tc0 : tc0 + P].bitcast(E4M3),
-                            lhsT_scale=x_q[a][1][:, tc0 : tc0 + P],
+                            lhsT=x_q[a][0][:, t0 : t0 + P].bitcast(E4M3),
+                            lhsT_scale=x_q[a][1][:, t0 : t0 + P],
                             rhs=dn_q[a][0][:, rt * P : (rt + 1) * P].bitcast(E4M3),
                             rhs_scale=dn_q[a][1][:, rt * P : (rt + 1) * P],
                             start=(a == 0),
@@ -153,19 +138,17 @@ def tile_mix_lorab_sgd_kernel(tc, x, dn, hs_words, hs_scales, dy0, dy1, prm, out
                 banks.append(bank)
             return banks
 
-        def h_quantize(b, banks, engine):
-            g = staged("h_g%d" % b)
-            for rt in range(r_tiles):
-                copy_on(engine, g[:, rt * P : (rt + 1) * P, :], banks[rt][:].rearrange("p (j r) -> p r j", j=PACK))
-            quantize(g, h_q[b], 0, E4M3)
-
         h_banks = [h_products(b) for b in range(2)]
-        h_quantize(0, h_banks[0], "vector")
-        h_quantize(1, h_banks[1], "scalar")
+        for b in range(2):
+            h_g = staged("h_g%d" % b)
+            for rt in range(R_TILES):
+                copies[b](h_g[:, rt * P : (rt + 1) * P, :], h_banks[b][rt][:].rearrange("p (j r) -> p r j", j=PACK))
+            quantize(h_g, h_q[b], 0, E4M3)
 
         acc = {}
 
-        def db_pass(rt, nb, g):
+        def db_pass(key, g):
+            rt, nb = key
             if g < 2:
                 lhsT = h_q[g][0][:, P * rt : P * (rt + 1)].bitcast(E4M3)
                 lhsT_scale = h_q[g][1][:, P * rt : P * (rt + 1)]
@@ -173,7 +156,7 @@ def tile_mix_lorab_sgd_kernel(tc, x, dn, hs_words, hs_scales, dy0, dy1, prm, out
                 lhsT = hs_w[g - 2][:, 2 * P * rt : 2 * P * (rt + 1)].bitcast(E2M1)
                 lhsT_scale = hs_sc[:, g - 2, P * rt : P * (rt + 1)]
             nc.tensor.matmul_mx(
-                out=acc[rt, nb][:],
+                out=acc[key][:],
                 lhsT=lhsT,
                 lhsT_scale=lhsT_scale,
                 rhs=dy_q[g][0][:, nb * BLK : (nb + 1) * BLK].bitcast(E5M2),
@@ -182,68 +165,71 @@ def tile_mix_lorab_sgd_kernel(tc, x, dn, hs_words, hs_scales, dy0, dy1, prm, out
                 stop=(g == 3),
             )
 
-        def copy_block(g_tile, src, c0, v_cols):
-            interleave("vector", g_tile[:, :v_cols, :], src[:, :, c0 : c0 + v_cols])
-            interleave("scalar", g_tile[:, v_cols:, :], src[:, :, c0 + v_cols : c0 + BLK])
+        def copy_block(dst, g, nb, v_cols):
+            c0 = nb * BLK
+            interleave(vector_copy, dst[:, :v_cols, :], dy_raw[g][:, :, c0 : c0 + v_cols])
+            interleave(scalar_copy, dst[:, v_cols:, :], dy_raw[g][:, :, c0 + v_cols : c0 + BLK])
 
-        def dy_pass(g, v_cols, after_block):
-            gs = [staged("dy_g%d%d" % (g, nb)) for nb in range(n_blocks)]
-            for nb in range(n_blocks + 1):
-                if nb < n_blocks:
-                    copy_block(gs[nb], dy_raw[g], nb * BLK, v_cols)
-                if nb > 0:
-                    quantize(gs[nb - 1], dy_q[g], (nb - 1) * BLK, E5M2)
-                    for rt, col in after_block[nb - 1]:
-                        db_pass(rt, col, g)
-
-        tiles = [(rt, nb) for rt in range(r_tiles) for nb in range(n_blocks)]
-        late = [(rt, nb) for rt, nb in tiles if rt >= 2 and nb >= 1]
-        resident = sorted([t for t in tiles if t not in late], key=lambda t: t[1])
-        bank_of = {}
+        resident = [(rt, 0) for rt in range(R_TILES)] + [(rt, nb) for nb in (1, 2) for rt in (0, 1)]
+        late = [(rt, nb) for rt in (2, 3) for nb in (1, 2)]
         for i, key in enumerate(resident):
-            bank_of[key] = i
             acc[key] = bank_tile(i, "acc%d%d" % key)
-        for g in range(2):
-            dy_pass(g, V_COLS, [[t for t in resident if t[1] == nb] for nb in range(n_blocks)])
-        dy_pass(2, V_COLS, [[], [], sorted(resident, key=lambda t: -t[1])])
-        gs = [staged("dy_g3%d" % nb) for nb in range(n_blocks)]
 
-        def close_block(nb):
-            quantize(gs[nb], dy_q[3], nb * BLK, E5M2)
-            for rt, col in resident:
-                if col == nb:
-                    db_pass(rt, col, 3)
+        def quantize_block(src, g, nb, keys):
+            quantize(src, dy_q[g], nb * BLK, E5M2)
+            for key in keys:
+                db_pass(key, g)
 
-        copy_block(gs[0], dy_raw[3], 0, V_COLS_FIRST)
-        close_block(0)
-        copy_block(gs[1], dy_raw[3], BLK, V_COLS_LAST)
-        copy_block(gs[2], dy_raw[3], 2 * BLK, V_COLS_LAST)
-        close_block(1)
-        close_block(2)
+        def in_block(nb):
+            return [key for key in resident if key[1] == nb]
+
+        for g in range(3):
+            dy_g = [staged("dy_g%d%d" % (g, nb)) for nb in range(N_BLOCKS)]
+            after = [in_block(nb) for nb in range(N_BLOCKS)] if g < 2 else [[], [], resident[::-1]]
+            for nb in range(N_BLOCKS + 1):
+                if nb < N_BLOCKS:
+                    copy_block(dy_g[nb], g, nb, V_COLS)
+                if nb > 0:
+                    quantize_block(dy_g[nb - 1], g, nb - 1, after[nb - 1])
+
+        def cols(nb):
+            return slice(nb * BLK, (nb + 1) * BLK)
+
+        def vector_finish(key):
+            dst = prm_t[key[0]][:, cols(key[1])]
+            nc.vector.scalar_tensor_tensor(out=dst, in0=acc[key][:], scalar=STEP, in1=dst, op0=ALU.mult, op1=ALU.add)
 
         part = {}
-        for rt in range(r_tiles):
-            part[rt] = keep.tile([P, BLK], F32, name="part%d" % rt)
-            nc.scalar.mul(out=part[rt][:], in_=acc[rt, 0][:], mul=STEP)
 
-        def finish(rt, nb):
-            cols = slice(nb * BLK, (nb + 1) * BLK)
-            if nb == 0:
-                nc.gpsimd.tensor_tensor(out=prm_t[rt][:, cols], in0=part[rt][:], in1=prm_t[rt][:, cols], op=ALU.add)
-            else:
-                nc.vector.scalar_tensor_tensor(
-                    out=prm_t[rt][:, cols], in0=acc[rt, nb][:], scalar=STEP, in1=prm_t[rt][:, cols], op0=ALU.mult, op1=ALU.add
-                )
+        def scalar_drain(key):
+            part[key] = keep.tile([P, BLK], F32, name="part%d%d" % key)
+            nc.scalar.mul(out=part[key][:], in_=acc[key][:], mul=STEP)
 
-        def row_tile_out(rt):
-            for nb in range(n_blocks):
-                finish(rt, nb)
-            (nc.sync, nc.scalar)[rt % 2].dma_start(out=out[rt * P : (rt + 1) * P, :], in_=prm_t[rt])
+        def gpsimd_finish(key):
+            dst = prm_t[key[0]][:, cols(key[1])]
+            nc.gpsimd.tensor_tensor(out=dst, in0=part[key][:], in1=dst, op=ALU.add)
 
-        row_tile_out(0)
-        for key, left in zip(late, [(rt, 0) for rt in range(r_tiles)]):
-            acc[key] = bank_tile(bank_of[left], "acc%d%d" % key)
+        def store(queue, rt, c0, c1):
+            queue.dma_start(out=out[rt * P : (rt + 1) * P, c0:c1], in_=prm_t[rt][:, c0:c1])
+
+        def late_tile(key, bank):
+            acc[key] = bank_tile(bank, "acc%d%d" % key)
             for g in range(4):
-                db_pass(key[0], key[1], g)
-        for rt in range(1, r_tiles):
-            row_tile_out(rt)
+                db_pass(key, g)
+
+        dy_g = [staged("dy_g3%d" % nb) for nb in range(N_BLOCKS)]
+        copy_block(dy_g[0], 3, 0, V_COLS_LAST[0])
+        quantize_block(dy_g[0], 3, 0, in_block(0))
+        copy_block(dy_g[1], 3, 1, V_COLS_LAST[1])
+        copy_block(dy_g[2], 3, 2, V_COLS_LAST[2])
+        quantize_block(dy_g[1], 3, 1, in_block(1))
+        quantize_block(dy_g[2], 3, 2, in_block(2))
+        for rt in range(R_TILES):
+            scalar_drain((rt, 0))
+        for bank, key in enumerate(late):
+            late_tile(key, bank)
+        for rt in range(R_TILES):
+            gpsimd_finish((rt, 0))
+            vector_finish((rt, 1))
+            vector_finish((rt, 2))
+            store((nc.sync, nc.scalar)[rt % 2], rt, 0, N)

@@ -116,8 +116,12 @@ def tile_mix_lorab_sgd_kernel(tc, x, dn, hs_words, hs_scales, dy0, dy1, prm, out
         nc.sync.dma_start(out=last[:, cut:], in_=last_rows[:, cut:])
         dy_raw.append(last[:].rearrange("p (j w) -> p j w", j=PACK))
         load_hs(1)
-        for rt in range(R_TILES):
-            nc.sync.dma_start(out=prm_t[rt][:], in_=prm[rt * P : (rt + 1) * P, :])
+
+        def load_prm(queue, rt):
+            queue.dma_start(out=prm_t[rt][:], in_=prm[rt * P : (rt + 1) * P, :])
+
+        for rt in (0, 2):
+            load_prm(nc.sync, rt)
 
         def h_products(b):
             banks = []
@@ -219,6 +223,8 @@ def tile_mix_lorab_sgd_kernel(tc, x, dn, hs_words, hs_scales, dy0, dy1, prm, out
 
         dy_g = [staged("dy_g3%d" % nb) for nb in range(N_BLOCKS)]
         copy_block(dy_g[0], 3, 0, V_COLS_LAST[0])
+        for rt in (1, 3):
+            load_prm(nc.scalar, rt)
         quantize_block(dy_g[0], 3, 0, in_block(0))
         copy_block(dy_g[1], 3, 1, V_COLS_LAST[1])
         copy_block(dy_g[2], 3, 2, V_COLS_LAST[2])

@@ -20,6 +20,7 @@ P = 128
 PACK = 4
 PASS = P * PACK
 BLK = 512
+HALF = BLK // 2
 N_BLOCKS = N // BLK
 R_TILES = R // P
 V_COLS = 256
@@ -152,7 +153,8 @@ def tile_mix_lorab_sgd_kernel(tc, x, dn, hs_words, hs_scales, dy0, dy1, prm, out
         acc = {}
 
         def db_pass(key, g):
-            rt, nb = key
+            rt, nb = key[:2]
+            c0, width = (nb * BLK, BLK) if len(key) == 2 else (nb * BLK + key[2] * HALF, HALF)
             if g < 2:
                 lhsT = h_q[g][0][:, P * rt : P * (rt + 1)].bitcast(E4M3)
                 lhsT_scale = h_q[g][1][:, P * rt : P * (rt + 1)]
@@ -160,11 +162,11 @@ def tile_mix_lorab_sgd_kernel(tc, x, dn, hs_words, hs_scales, dy0, dy1, prm, out
                 lhsT = hs_w[g - 2][:, 2 * P * rt : 2 * P * (rt + 1)].bitcast(E2M1)
                 lhsT_scale = hs_sc[:, g - 2, P * rt : P * (rt + 1)]
             nc.tensor.matmul_mx(
-                out=acc[key][:],
+                out=acc[key][:, :width],
                 lhsT=lhsT,
                 lhsT_scale=lhsT_scale,
-                rhs=dy_q[g][0][:, nb * BLK : (nb + 1) * BLK].bitcast(E5M2),
-                rhs_scale=dy_q[g][1][:, nb * BLK : (nb + 1) * BLK],
+                rhs=dy_q[g][0][:, c0 : c0 + width].bitcast(E5M2),
+                rhs_scale=dy_q[g][1][:, c0 : c0 + width],
                 start=(g == 0),
                 stop=(g == 3),
             )
@@ -217,7 +219,7 @@ def tile_mix_lorab_sgd_kernel(tc, x, dn, hs_words, hs_scales, dy0, dy1, prm, out
             queue.dma_start(out=out[rt * P : (rt + 1) * P, c0:c1], in_=prm_t[rt][:, c0:c1])
 
         def late_tile(key, bank):
-            acc[key] = bank_tile(bank, "acc%d%d" % key)
+            acc[key] = bank_tile(bank, "late%d" % bank)
             for g in range(4):
                 db_pass(key, g)
 
@@ -232,10 +234,22 @@ def tile_mix_lorab_sgd_kernel(tc, x, dn, hs_words, hs_scales, dy0, dy1, prm, out
         quantize_block(dy_g[2], 3, 2, in_block(2))
         for rt in range(R_TILES):
             scalar_drain((rt, 0))
-        for bank, key in enumerate(late):
+        for bank, key in enumerate(late[:3]):
             late_tile(key, bank)
+        late_tile((3, 2, 0), 3)
         for rt in range(R_TILES):
             gpsimd_finish((rt, 0))
+            if rt == 0:
+                store(nc.sync, rt, 0, BLK)
             vector_finish((rt, 1))
-            vector_finish((rt, 2))
-            store((nc.sync, nc.scalar)[rt % 2], rt, 0, N)
+            if rt == 0:
+                late_tile((3, 2, 1), 4)
+            if rt < 3:
+                vector_finish((rt, 2))
+            else:
+                for u in range(2):
+                    dst = prm_t[rt][:, 2 * BLK + u * HALF : 2 * BLK + (u + 1) * HALF]
+                    nc.vector.scalar_tensor_tensor(
+                        out=dst, in0=acc[rt, 2, u][:, :HALF], scalar=STEP, in1=dst, op0=ALU.mult, op1=ALU.add
+                    )
+            store((nc.sync, nc.scalar)[rt % 2], rt, BLK if rt == 0 else 0, N)

@@ -10,6 +10,7 @@ F32 = mybir.dt.float32
 BF16 = mybir.dt.bfloat16
 I32 = mybir.dt.int32
 U32 = mybir.dt.uint32
+U16 = mybir.dt.uint16
 U8 = mybir.dt.uint8
 E4M3 = mybir.dt.float8_e4m3fn_x4
 E5M2 = mybir.dt.float8_e5m2_x4
@@ -23,8 +24,10 @@ BLK = 512
 HALF = BLK // 2
 N_BLOCKS = N // BLK
 R_TILES = R // P
+LINE = 8
 V_COLS = 256
-V_COLS_LAST = (336, 256, 256)
+V_COLS_LAST = (192, 304, 304)
+PRM_CUTS = (0, 4 * BLK, 8 * BLK, 12 * BLK)
 
 
 def tile_mix_lorab_sgd_kernel(tc, x, dn, hs_words, hs_scales, dy0, dy1, prm, out):
@@ -37,10 +40,12 @@ def tile_mix_lorab_sgd_kernel(tc, x, dn, hs_words, hs_scales, dy0, dy1, prm, out
         psum = ctx.enter_context(tc.psum_pool(name="psum", bufs=1))
         ctx.enter_context(tc.manual_schedule())
 
+        def runs(rows):
+            return rows.rearrange("(p j) w -> p (j w)", j=PACK)
+
         def load_pass(queue, src, a, name, slot):
-            width = src.shape[1]
-            t = raw.tile([P, PACK * width], F32, name=name, tag=slot, align_bytes=256)
-            queue.dma_start(out=t[:], in_=src[a * PASS : (a + 1) * PASS, :].rearrange("(p j) w -> p (j w)", j=PACK))
+            t = raw.tile([P, PACK * src.shape[1]], F32, name=name, tag=slot, align_bytes=256)
+            queue.dma_start(out=t[:], in_=runs(src[a * PASS : (a + 1) * PASS, :]))
             return t[:].rearrange("p (j w) -> p j w", j=PACK)
 
         def planes(name, width):
@@ -60,33 +65,52 @@ def tile_mix_lorab_sgd_kernel(tc, x, dn, hs_words, hs_scales, dy0, dy1, prm, out
         def interleave(copy, dst, src):
             copy(dst.rearrange("p (c i) j -> p c j i", i=4), src.rearrange("p j (c i) -> p c j i", i=4))
 
+        def interleave_dealt(copy, dst, src):
+            copy(dst.rearrange("p (t m) j -> p m j t", t=PACK), src.rearrange("p j (m t) -> p m j t", t=PACK))
+
         def quantize(g, plane, col0, fmt):
             codes, scales = plane
+            width = g.shape[1]
             nc.vector.quantize_mx(
-                out=codes[:, col0 : col0 + BLK].bitcast(fmt),
-                scales=scales[:, col0 : col0 + BLK],
-                in_=g[:].rearrange("p w j -> p (w j)"),
+                out=codes[:, col0 : col0 + width].bitcast(fmt),
+                scales=scales[:, col0 : col0 + width],
+                in_=g.rearrange("p w j -> p (w j)"),
             )
 
         def bank_tile(i, name):
             return psum.tile([P, BLK], F32, name=name, tag="bank%d" % i)
 
-        hs_sc = keep.tile([P, 2, R], U8, name="hs_sc", align_bytes=256)
-        hs_w = [keep.tile([P, 2 * R], U8, name="hs_w%d" % a, align_bytes=256) for a in range(2)]
-        prm_t = [keep.tile([P, N], F32, name="prm%d" % rt, align_bytes=256) for rt in range(R_TILES)]
+        hs_sc_in = keep.tile([P, 2, R], U8, name="hs_sc_in", align_bytes=256)
+        hs_sc = keep.tile([P, 2, R], U8, name="hs_sc", align_bytes=64)
+        hs_w_in = [keep.tile([P, 2 * R], U8, name="hs_w_in%d" % a, align_bytes=256) for a in range(2)]
+        hs_w = [keep.tile([P, 2 * R], U8, name="hs_w%d" % a, align_bytes=64) for a in range(2)]
+        prm_t = keep.tile([P, R_TILES * N], F32, name="prm_t", align_bytes=256)
 
         def load_hs(a):
-            nc.sync.dma_start(out=hs_w[a][:].bitcast(I32), in_=hs_words[a].bitcast(I32))
+            nc.sync.dma_start(out=hs_w_in[a][:].bitcast(I32), in_=hs_words[a].bitcast(I32))
 
+        def load_scale_rows(queue, r, passes):
+            queue.dma_start(
+                out=hs_sc_in[r:P:32, passes, :].bitcast(I32),
+                in_=hs_scales[passes, r:16:4, :].rearrange("a q n -> q a n").bitcast(I32),
+            )
+
+        def deal_hs(a):
+            scalar_copy(
+                hs_w[a][:].bitcast(U16).rearrange("p (t c i) -> p c t i", t=PACK, i=LINE),
+                hs_w_in[a][:].bitcast(U16).rearrange("p (c i t) -> p c t i", t=PACK, i=LINE),
+            )
+
+        nc.gpsimd.memset(hs_sc_in[:].bitcast(I32), 0)
         dn_raw = [load_pass(nc.scalar, dn, a, "dn_raw%d" % a, slot) for a, slot in enumerate(("slot_b", "slot_f"))]
         x_raw = [load_pass(nc.sync, x, a, "x_raw%d" % a, slot) for a, slot in enumerate(("slot_a", "slot_g"))]
-        for r in range(4):
-            nc.scalar.dma_start(
-                out=hs_sc[r:P:32, :, :].bitcast(I32),
-                in_=hs_scales[:, r:16:4, :].rearrange("a q n -> q a n").bitcast(I32),
-            )
+        for r in range(3):
+            load_scale_rows(nc.scalar, r, slice(0, 2))
+        load_scale_rows(nc.scalar, 3, slice(0, 1))
         load_hs(0)
-        dy_raw = [load_pass(nc.sync, dy1, 0, "dy1_raw0", "slot_c"), load_pass(nc.scalar, dy1, 1, "dy1_raw1", "slot_e")]
+        dy1_second = load_pass(nc.sync, dy1, 1, "dy1_raw1", "slot_c")
+        dy_raw = [load_pass(nc.scalar, dy1, 0, "dy1_raw0", "slot_e"), dy1_second]
+        load_scale_rows(nc.sync, 3, slice(1, 2))
 
         x_q = [planes("x%d" % a, T) for a in range(2)]
         dn_q = [planes("dn%d" % a, R) for a in range(2)]
@@ -94,35 +118,26 @@ def tile_mix_lorab_sgd_kernel(tc, x, dn, hs_words, hs_scales, dy0, dy1, prm, out
         dy_q = [planes("dy%d" % g, N) for g in range(4)]
         copies = (vector_copy, scalar_copy)
 
-        dn_g = [staged("dn_g%d" % a) for a in range(2)]
         for a in range(2):
-            interleave(copies[a], dn_g[a][:], dn_raw[a])
-        for a in range(2):
-            quantize(dn_g[a], dn_q[a], 0, E4M3)
-        for b in range(2):
-            x_g = [staged("x_g%d%d" % (a, b)) for a in range(2)]
-            for a in range(2):
-                copies[a](
-                    x_g[a][:].rearrange("p (t m) j -> p m j t", t=PACK),
-                    x_raw[a][:, :, b * BLK : (b + 1) * BLK].rearrange("p j (m t) -> p m j t", t=PACK),
-                )
-            for a in range(2):
-                quantize(x_g[a], x_q[a], b * BLK, E4M3)
+            dn_g = staged("dn_g%d" % a)
+            interleave_dealt(copies[a], dn_g[:], dn_raw[a])
+            x_g = [staged("x_g%d%d" % (a, b)) for b in range(2)]
+            for b in range(2):
+                interleave_dealt(vector_copy, x_g[b][:], x_raw[a][:, :, b * BLK : (b + 1) * BLK])
+            quantize(dn_g[:], dn_q[a], 0, E4M3)
+            for b in range(2):
+                quantize(x_g[b][:], x_q[a], b * BLK, E4M3)
 
         dy_raw.append(load_pass(nc.sync, dy0, 0, "dy0_raw0", "slot_a"))
         last = raw.tile([P, PACK * N], F32, name="dy0_raw1", tag="slot_b", align_bytes=256)
-        last_rows = dy0[PASS:, :].rearrange("(p j) w -> p (j w)", j=PACK)
+        last_rows = runs(dy0[PASS:, :])
         cut = (PACK - 1) * N + BLK
         nc.sync.dma_start(out=last[:, :cut], in_=last_rows[:, :cut])
+        load_hs(1)
         nc.sync.dma_start(out=last[:, cut:], in_=last_rows[:, cut:])
         dy_raw.append(last[:].rearrange("p (j w) -> p j w", j=PACK))
-        load_hs(1)
-
-        def load_prm(queue, rt):
-            queue.dma_start(out=prm_t[rt][:], in_=prm[rt * P : (rt + 1) * P, :])
-
-        for rt in (0, 2):
-            load_prm(nc.sync, rt)
+        for c0, c1 in zip(PRM_CUTS, PRM_CUTS[1:]):
+            nc.sync.dma_start(out=prm_t[:, c0:c1], in_=runs(prm)[:, c0:c1])
 
         def h_products(b):
             banks = []
@@ -144,17 +159,22 @@ def tile_mix_lorab_sgd_kernel(tc, x, dn, hs_words, hs_scales, dy0, dy1, prm, out
             return banks
 
         h_banks = [h_products(b) for b in range(2)]
+        deal_hs(0)
         for b in range(2):
             h_g = staged("h_g%d" % b)
             for rt in range(R_TILES):
                 copies[b](h_g[:, rt * P : (rt + 1) * P, :], h_banks[b][rt][:].rearrange("p (j r) -> p r j", j=PACK))
-            quantize(h_g, h_q[b], 0, E4M3)
+            quantize(h_g[:], h_q[b], 0, E4M3)
 
         acc = {}
 
-        def db_pass(key, g):
+        def db_pass(key, g, half=None):
             rt, nb = key[:2]
             c0, width = (nb * BLK, BLK) if len(key) == 2 else (nb * BLK + key[2] * HALF, HALF)
+            p0 = 0
+            if half is not None:
+                p0, width = half * HALF, HALF
+                c0 = c0 + p0
             if g < 2:
                 lhsT = h_q[g][0][:, P * rt : P * (rt + 1)].bitcast(E4M3)
                 lhsT_scale = h_q[g][1][:, P * rt : P * (rt + 1)]
@@ -162,19 +182,22 @@ def tile_mix_lorab_sgd_kernel(tc, x, dn, hs_words, hs_scales, dy0, dy1, prm, out
                 lhsT = hs_w[g - 2][:, 2 * P * rt : 2 * P * (rt + 1)].bitcast(E2M1)
                 lhsT_scale = hs_sc[:, g - 2, P * rt : P * (rt + 1)]
             nc.tensor.matmul_mx(
-                out=acc[key][:, :width],
+                out=acc[key][:, p0 : p0 + width],
                 lhsT=lhsT,
                 lhsT_scale=lhsT_scale,
                 rhs=dy_q[g][0][:, c0 : c0 + width].bitcast(E5M2),
                 rhs_scale=dy_q[g][1][:, c0 : c0 + width],
                 start=(g == 0),
-                stop=(g == 3),
+                stop=(g == 3 and half != 0),
             )
 
-        def copy_block(dst, g, nb, v_cols):
-            c0 = nb * BLK
+        def copy_columns(dst, g, c0, v_cols):
+            width = dst.shape[1]
             interleave(vector_copy, dst[:, :v_cols, :], dy_raw[g][:, :, c0 : c0 + v_cols])
-            interleave(scalar_copy, dst[:, v_cols:, :], dy_raw[g][:, :, c0 + v_cols : c0 + BLK])
+            interleave(scalar_copy, dst[:, v_cols:, :], dy_raw[g][:, :, c0 + v_cols : c0 + width])
+
+        def copy_block(dst, g, nb, v_cols):
+            copy_columns(dst[:], g, nb * BLK, v_cols)
 
         resident = [(rt, 0) for rt in range(R_TILES)] + [(rt, nb) for nb in (1, 2) for rt in (0, 1)]
         late = [(rt, nb) for rt in (2, 3) for nb in (1, 2)]
@@ -182,7 +205,7 @@ def tile_mix_lorab_sgd_kernel(tc, x, dn, hs_words, hs_scales, dy0, dy1, prm, out
             acc[key] = bank_tile(i, "acc%d%d" % key)
 
         def quantize_block(src, g, nb, keys):
-            quantize(src, dy_q[g], nb * BLK, E5M2)
+            quantize(src[:], dy_q[g], nb * BLK, E5M2)
             for key in keys:
                 db_pass(key, g)
 
@@ -190,20 +213,28 @@ def tile_mix_lorab_sgd_kernel(tc, x, dn, hs_words, hs_scales, dy0, dy1, prm, out
             return [key for key in resident if key[1] == nb]
 
         for g in range(3):
+            if g == 2:
+                vector_copy(
+                    hs_sc[:].rearrange("p a (t m) -> p a t m", t=PACK),
+                    hs_sc_in[:].rearrange("p a (m t) -> p a t m", t=PACK),
+                )
             dy_g = [staged("dy_g%d%d" % (g, nb)) for nb in range(N_BLOCKS)]
-            after = [in_block(nb) for nb in range(N_BLOCKS)] if g < 2 else [[], [], resident[::-1]]
-            for nb in range(N_BLOCKS + 1):
-                if nb < N_BLOCKS:
-                    copy_block(dy_g[nb], g, nb, V_COLS)
-                if nb > 0:
-                    quantize_block(dy_g[nb - 1], g, nb - 1, after[nb - 1])
+            order = list(range(N_BLOCKS))[::-1]
+            for i in range(N_BLOCKS + 1):
+                if i < N_BLOCKS:
+                    copy_block(dy_g[order[i]], g, order[i], V_COLS)
+                if i > 0:
+                    quantize_block(dy_g[order[i - 1]], g, order[i - 1], in_block(order[i - 1]))
 
-        def cols(nb):
-            return slice(nb * BLK, (nb + 1) * BLK)
+        def result(rt, c0, width):
+            return prm_t[:, rt * N + c0 : rt * N + c0 + width]
 
         def vector_finish(key):
-            dst = prm_t[key[0]][:, cols(key[1])]
-            nc.vector.scalar_tensor_tensor(out=dst, in0=acc[key][:], scalar=STEP, in1=dst, op0=ALU.mult, op1=ALU.add)
+            c0, width = (key[1] * BLK, BLK) if len(key) == 2 else (key[1] * BLK + key[2] * HALF, HALF)
+            dst = result(key[0], c0, width)
+            nc.vector.scalar_tensor_tensor(
+                out=dst, in0=acc[key][:, :width], scalar=STEP, in1=dst, op0=ALU.mult, op1=ALU.add
+            )
 
         part = {}
 
@@ -212,11 +243,8 @@ def tile_mix_lorab_sgd_kernel(tc, x, dn, hs_words, hs_scales, dy0, dy1, prm, out
             nc.scalar.mul(out=part[key][:], in_=acc[key][:], mul=STEP)
 
         def gpsimd_finish(key):
-            dst = prm_t[key[0]][:, cols(key[1])]
+            dst = result(key[0], key[1] * BLK, BLK)
             nc.gpsimd.tensor_tensor(out=dst, in0=part[key][:], in1=dst, op=ALU.add)
-
-        def store(queue, rt, c0, c1):
-            queue.dma_start(out=out[rt * P : (rt + 1) * P, c0:c1], in_=prm_t[rt][:, c0:c1])
 
         def late_tile(key, bank):
             acc[key] = bank_tile(bank, "late%d" % bank)
@@ -224,10 +252,14 @@ def tile_mix_lorab_sgd_kernel(tc, x, dn, hs_words, hs_scales, dy0, dy1, prm, out
                 db_pass(key, g)
 
         dy_g = [staged("dy_g3%d" % nb) for nb in range(N_BLOCKS)]
-        copy_block(dy_g[0], 3, 0, V_COLS_LAST[0])
-        for rt in (1, 3):
-            load_prm(nc.scalar, rt)
-        quantize_block(dy_g[0], 3, 0, in_block(0))
+        halves = [dy_g[0][:, u * HALF : (u + 1) * HALF, :] for u in range(2)]
+        for u in range(2):
+            copy_columns(halves[u], 3, u * HALF, V_COLS_LAST[0])
+        deal_hs(1)
+        for u in range(2):
+            quantize(halves[u], dy_q[3], u * HALF, E5M2)
+            for key in in_block(0):
+                db_pass(key, 3, u)
         copy_block(dy_g[1], 3, 1, V_COLS_LAST[1])
         copy_block(dy_g[2], 3, 2, V_COLS_LAST[2])
         quantize_block(dy_g[1], 3, 1, in_block(1))
@@ -239,8 +271,6 @@ def tile_mix_lorab_sgd_kernel(tc, x, dn, hs_words, hs_scales, dy0, dy1, prm, out
         late_tile((3, 2, 0), 3)
         for rt in range(R_TILES):
             gpsimd_finish((rt, 0))
-            if rt == 0:
-                store(nc.sync, rt, 0, BLK)
             vector_finish((rt, 1))
             if rt == 0:
                 late_tile((3, 2, 1), 4)
@@ -248,8 +278,5 @@ def tile_mix_lorab_sgd_kernel(tc, x, dn, hs_words, hs_scales, dy0, dy1, prm, out
                 vector_finish((rt, 2))
             else:
                 for u in range(2):
-                    dst = prm_t[rt][:, 2 * BLK + u * HALF : 2 * BLK + (u + 1) * HALF]
-                    nc.vector.scalar_tensor_tensor(
-                        out=dst, in0=acc[rt, 2, u][:, :HALF], scalar=STEP, in1=dst, op0=ALU.mult, op1=ALU.add
-                    )
-            store((nc.sync, nc.scalar)[rt % 2], rt, BLK if rt == 0 else 0, N)
+                    vector_finish((rt, 2, u))
+            (nc.sync, nc.scalar)[rt % 2].dma_start(out=runs(out)[:, rt * N : (rt + 1) * N], in_=result(rt, 0, N))

@@ -26,7 +26,7 @@ N_BLOCKS = N // BLK
 R_TILES = R // P
 LINE = 8
 V_COLS = 256
-V_COLS_LAST = (192, 304, 304)
+V_COLS_LAST = (192, 280, 280)
 PRM_CUTS = (0, 4 * BLK, 8 * BLK, 12 * BLK)
 
 

@@ -19,15 +19,16 @@ ALU = mybir.AluOpType
 
 P = 128
 PACK = 4
-PASS = P * PACK
 BLK = 512
 HALF = BLK // 2
 N_BLOCKS = N // BLK
 R_TILES = R // P
 LINE = 8
+QUAD = 32
 V_COLS = 256
-V_COLS_LAST = (192, 280, 280)
-PRM_CUTS = (0, 4 * BLK, 8 * BLK, 12 * BLK)
+V_COLS_HALF = 144
+V_COLS_LAST = 272
+PRM_LOADS = 3
 
 
 def tile_mix_lorab_sgd_kernel(tc, x, dn, hs_words, hs_scales, dy0, dy1, prm, out):
@@ -40,13 +41,14 @@ def tile_mix_lorab_sgd_kernel(tc, x, dn, hs_words, hs_scales, dy0, dy1, prm, out
         psum = ctx.enter_context(tc.psum_pool(name="psum", bufs=1))
         ctx.enter_context(tc.manual_schedule())
 
-        def runs(rows):
-            return rows.rearrange("(p j) w -> p (j w)", j=PACK)
+        def by_pass(rows):
+            return rows.rearrange("(a p j) w -> p a (j w)", p=P, j=PACK)
 
-        def load_pass(queue, src, a, name, slot):
-            t = raw.tile([P, PACK * src.shape[1]], F32, name=name, tag=slot, align_bytes=256)
-            queue.dma_start(out=t[:], in_=runs(src[a * PASS : (a + 1) * PASS, :]))
-            return t[:].rearrange("p (j w) -> p j w", j=PACK)
+        def load_passes(src, name, slot):
+            view = by_pass(src)
+            t = raw.tile(list(view.shape), F32, name=name, tag=slot, align_bytes=256)
+            nc.sync.dma_start(out=t[:], in_=view)
+            return [t[:, a, :].rearrange("p (j w) -> p j w", j=PACK) for a in range(view.shape[1])]
 
         def planes(name, width):
             codes = keep.tile([P, width], U32, name=name + "_codes", align_bytes=64)
@@ -61,6 +63,8 @@ def tile_mix_lorab_sgd_kernel(tc, x, dn, hs_words, hs_scales, dy0, dy1, prm, out
 
         def scalar_copy(dst, src):
             nc.scalar.copy(out=dst, in_=src)
+
+        copies = (vector_copy, scalar_copy)
 
         def interleave(copy, dst, src):
             copy(dst.rearrange("p (c i) j -> p c j i", i=4), src.rearrange("p j (c i) -> p c j i", i=4))
@@ -80,64 +84,67 @@ def tile_mix_lorab_sgd_kernel(tc, x, dn, hs_words, hs_scales, dy0, dy1, prm, out
         def bank_tile(i, name):
             return psum.tile([P, BLK], F32, name=name, tag="bank%d" % i)
 
-        hs_sc_in = keep.tile([P, 2, R], U8, name="hs_sc_in", align_bytes=256)
+        sc_in = keep.tile([P, 5, R], U8, name="sc_in", align_bytes=256)
         hs_sc = keep.tile([P, 2, R], U8, name="hs_sc", align_bytes=64)
-        hs_w_in = [keep.tile([P, 2 * R], U8, name="hs_w_in%d" % a, align_bytes=256) for a in range(2)]
-        hs_w = [keep.tile([P, 2 * R], U8, name="hs_w%d" % a, align_bytes=64) for a in range(2)]
+        hs_in = keep.tile([P, 2, 2 * R], U8, name="hs_in", align_bytes=256)
+        hs_w = keep.tile([P, 2, 2 * R], U8, name="hs_w", align_bytes=64)
         prm_t = keep.tile([P, R_TILES * N], F32, name="prm_t", align_bytes=256)
+        sc_words = sc_in[:].bitcast(I32)
 
-        def load_hs(a):
-            nc.sync.dma_start(out=hs_w_in[a][:].bitcast(I32), in_=hs_words[a].bitcast(I32))
+        nc.gpsimd.memset(sc_words, 0)
+        x_raw = load_passes(x, "x_raw", "first")
+        nc.scalar.dma_start(out=hs_in[:].bitcast(I32), in_=hs_words.rearrange("a p c -> p a c").bitcast(I32))
+        sc_rows = hs_scales.rearrange("a (h u j) n -> u j (a h) n", u=2, j=4).bitcast(I32)
+        nc.sync.dma_start(out=sc_words[0:4, 1:5, :], in_=sc_rows[0])
+        nc.sync.dma_start(out=sc_words[3 * QUAD : 3 * QUAD + 4, 0:4, :], in_=sc_rows[1])
+        dn_raw = load_passes(dn, "dn_raw", "dn")
+        dy_raw = load_passes(dy1, "dy1_raw", "dy1")
 
-        def load_scale_rows(queue, r, passes):
-            queue.dma_start(
-                out=hs_sc_in[r:P:32, passes, :].bitcast(I32),
-                in_=hs_scales[passes, r:16:4, :].rearrange("a q n -> q a n").bitcast(I32),
-            )
-
-        def deal_hs(a):
+        for a in range(2):
             scalar_copy(
-                hs_w[a][:].bitcast(U16).rearrange("p (t c i) -> p c t i", t=PACK, i=LINE),
-                hs_w_in[a][:].bitcast(U16).rearrange("p (c i t) -> p c t i", t=PACK, i=LINE),
+                hs_w[:, a, :].bitcast(U16).rearrange("p (t c i) -> p c t i", t=PACK, i=LINE),
+                hs_in[:, a, :].bitcast(U16).rearrange("p (c i t) -> p c t i", t=PACK, i=LINE),
             )
-
-        nc.gpsimd.memset(hs_sc_in[:].bitcast(I32), 0)
-        dn_raw = [load_pass(nc.scalar, dn, a, "dn_raw%d" % a, slot) for a, slot in enumerate(("slot_b", "slot_f"))]
-        x_raw = [load_pass(nc.sync, x, a, "x_raw%d" % a, slot) for a, slot in enumerate(("slot_a", "slot_g"))]
-        for r in range(3):
-            load_scale_rows(nc.scalar, r, slice(0, 2))
-        load_scale_rows(nc.scalar, 3, slice(0, 1))
-        load_hs(0)
-        dy1_second = load_pass(nc.sync, dy1, 1, "dy1_raw1", "slot_c")
-        dy_raw = [load_pass(nc.scalar, dy1, 0, "dy1_raw0", "slot_e"), dy1_second]
-        load_scale_rows(nc.sync, 3, slice(1, 2))
 
         x_q = [planes("x%d" % a, T) for a in range(2)]
         dn_q = [planes("dn%d" % a, R) for a in range(2)]
         h_q = [planes("h%d" % b, R) for b in range(2)]
         dy_q = [planes("dy%d" % g, N) for g in range(4)]
-        copies = (vector_copy, scalar_copy)
 
-        for a in range(2):
-            dn_g = staged("dn_g%d" % a)
-            interleave_dealt(copies[a], dn_g[:], dn_raw[a])
-            x_g = [staged("x_g%d%d" % (a, b)) for b in range(2)]
-            for b in range(2):
-                interleave_dealt(vector_copy, x_g[b][:], x_raw[a][:, :, b * BLK : (b + 1) * BLK])
-            quantize(dn_g[:], dn_q[a], 0, E4M3)
-            for b in range(2):
-                quantize(x_g[b][:], x_q[a], b * BLK, E4M3)
+        x_g = {}
+        for b in range(2):
+            for a in range(2):
+                x_g[a, b] = staged("x_g%d%d" % (a, b))
+                interleave_dealt(copies[a], x_g[a, b][:], x_raw[a][:, :, b * BLK : (b + 1) * BLK])
+        for b in range(2):
+            for a in range(2):
+                quantize(x_g[a, b][:], x_q[a], b * BLK, E4M3)
 
-        dy_raw.append(load_pass(nc.sync, dy0, 0, "dy0_raw0", "slot_a"))
-        last = raw.tile([P, PACK * N], F32, name="dy0_raw1", tag="slot_b", align_bytes=256)
-        last_rows = runs(dy0[PASS:, :])
+        dy_raw.extend(load_passes(dy0[: P * PACK, :], "dy0_raw0", "first"))
+        last = raw.tile([P, PACK * N], F32, name="dy0_raw1", tag="last", align_bytes=256)
+        last_rows = by_pass(dy0)[:, 1, :]
         cut = (PACK - 1) * N + BLK
         nc.sync.dma_start(out=last[:, :cut], in_=last_rows[:, :cut])
-        load_hs(1)
         nc.sync.dma_start(out=last[:, cut:], in_=last_rows[:, cut:])
         dy_raw.append(last[:].rearrange("p (j w) -> p j w", j=PACK))
-        for c0, c1 in zip(PRM_CUTS, PRM_CUTS[1:]):
-            nc.sync.dma_start(out=prm_t[:, c0:c1], in_=runs(prm)[:, c0:c1])
+        prm_rows = by_pass(prm)[:, 0, :]
+        third = R_TILES * N // PRM_LOADS
+        for c0 in range(0, R_TILES * N, third):
+            nc.sync.dma_start(out=prm_t[:, c0 : c0 + third], in_=prm_rows[:, c0 : c0 + third])
+
+        dn_g = [staged("dn_g%d" % a) for a in range(2)]
+        for a in range(2):
+            interleave_dealt(copies[a], dn_g[a][:], dn_raw[a])
+        for a in range(2):
+            quantize(dn_g[a][:], dn_q[a], 0, E4M3)
+
+        for a in range(2):
+            vector_copy(sc_words[2 * QUAD : 2 * QUAD + 4, 1 + 2 * a, :], sc_words[0:4, 2 + 2 * a, :])
+            vector_copy(sc_words[QUAD : 2 * QUAD, 1 + 2 * a, :], sc_words[3 * QUAD :, 2 * a, :])
+        vector_copy(
+            hs_sc[:].rearrange("p a (t m) -> p a t m", t=PACK),
+            sc_in[:, 1:5:2, :].rearrange("p a (m t) -> p a t m", t=PACK),
+        )
 
         def h_products(b):
             banks = []
@@ -159,16 +166,17 @@ def tile_mix_lorab_sgd_kernel(tc, x, dn, hs_words, hs_scales, dy0, dy1, prm, out
             return banks
 
         h_banks = [h_products(b) for b in range(2)]
-        deal_hs(0)
         for b in range(2):
             h_g = staged("h_g%d" % b)
             for rt in range(R_TILES):
-                copies[b](h_g[:, rt * P : (rt + 1) * P, :], h_banks[b][rt][:].rearrange("p (j r) -> p r j", j=PACK))
+                copies[rt % 2](
+                    h_g[:, rt * P : (rt + 1) * P, :], h_banks[b][rt][:].rearrange("p (j r) -> p r j", j=PACK)
+                )
             quantize(h_g[:], h_q[b], 0, E4M3)
 
         acc = {}
 
-        def db_pass(key, g, half=None):
+        def db_pass(key, g, half=None, first=0, final=3):
             rt, nb = key[:2]
             c0, width = (nb * BLK, BLK) if len(key) == 2 else (nb * BLK + key[2] * HALF, HALF)
             p0 = 0
@@ -179,7 +187,7 @@ def tile_mix_lorab_sgd_kernel(tc, x, dn, hs_words, hs_scales, dy0, dy1, prm, out
                 lhsT = h_q[g][0][:, P * rt : P * (rt + 1)].bitcast(E4M3)
                 lhsT_scale = h_q[g][1][:, P * rt : P * (rt + 1)]
             else:
-                lhsT = hs_w[g - 2][:, 2 * P * rt : 2 * P * (rt + 1)].bitcast(E2M1)
+                lhsT = hs_w[:, g - 2, 2 * P * rt : 2 * P * (rt + 1)].bitcast(E2M1)
                 lhsT_scale = hs_sc[:, g - 2, P * rt : P * (rt + 1)]
             nc.tensor.matmul_mx(
                 out=acc[key][:, p0 : p0 + width],
@@ -187,8 +195,8 @@ def tile_mix_lorab_sgd_kernel(tc, x, dn, hs_words, hs_scales, dy0, dy1, prm, out
                 lhsT_scale=lhsT_scale,
                 rhs=dy_q[g][0][:, c0 : c0 + width].bitcast(E5M2),
                 rhs_scale=dy_q[g][1][:, c0 : c0 + width],
-                start=(g == 0),
-                stop=(g == 3 and half != 0),
+                start=(g == first),
+                stop=(g == final and half != 0),
             )
 
         def copy_columns(dst, g, c0, v_cols):
@@ -196,35 +204,39 @@ def tile_mix_lorab_sgd_kernel(tc, x, dn, hs_words, hs_scales, dy0, dy1, prm, out
             interleave(vector_copy, dst[:, :v_cols, :], dy_raw[g][:, :, c0 : c0 + v_cols])
             interleave(scalar_copy, dst[:, v_cols:, :], dy_raw[g][:, :, c0 + v_cols : c0 + width])
 
-        def copy_block(dst, g, nb, v_cols):
-            copy_columns(dst[:], g, nb * BLK, v_cols)
-
-        resident = [(rt, 0) for rt in range(R_TILES)] + [(rt, nb) for nb in (1, 2) for rt in (0, 1)]
-        late = [(rt, nb) for rt in (2, 3) for nb in (1, 2)]
+        parked, successor = (3, 2), (1, 2)
+        resident = [(rt, 0) for rt in range(R_TILES)] + [(0, 1), (1, 1), (0, 2), parked]
         for i, key in enumerate(resident):
             acc[key] = bank_tile(i, "acc%d%d" % key)
-
-        def quantize_block(src, g, nb, keys):
-            quantize(src[:], dy_q[g], nb * BLK, E5M2)
-            for key in keys:
-                db_pass(key, g)
 
         def in_block(nb):
             return [key for key in resident if key[1] == nb]
 
+        def quantize_block(src, g, nb):
+            quantize(src[:], dy_q[g], nb * BLK, E5M2)
+            for key in in_block(nb):
+                db_pass(key, g, final=2 if key == parked else 3)
+
+        part = {}
+
+        def scalar_drain(key):
+            part[key] = keep.tile([P, BLK], F32, name="part%d%d" % key)
+            nc.scalar.mul(out=part[key][:], in_=acc[key][:], mul=STEP)
+
+        steps = [(g, nb) for g in range(3) for nb in reversed(range(N_BLOCKS))]
+        before = None
+        for g, nb in steps:
+            dy_g = staged("dy_g%d%d" % (g, nb))
+            copy_columns(dy_g[:], g, nb * BLK, V_COLS)
+            if before is not None:
+                quantize_block(*before)
+            before = (dy_g, g, nb)
+        scalar_drain(parked)
+        quantize_block(*before)
+        resident[-1:] = [successor]
+        acc[successor] = bank_tile(len(resident) - 1, "acc%d%d" % successor)
         for g in range(3):
-            if g == 2:
-                vector_copy(
-                    hs_sc[:].rearrange("p a (t m) -> p a t m", t=PACK),
-                    hs_sc_in[:].rearrange("p a (m t) -> p a t m", t=PACK),
-                )
-            dy_g = [staged("dy_g%d%d" % (g, nb)) for nb in range(N_BLOCKS)]
-            order = list(range(N_BLOCKS))[::-1]
-            for i in range(N_BLOCKS + 1):
-                if i < N_BLOCKS:
-                    copy_block(dy_g[order[i]], g, order[i], V_COLS)
-                if i > 0:
-                    quantize_block(dy_g[order[i - 1]], g, order[i - 1], in_block(order[i - 1]))
+            db_pass(successor, g)
 
         def result(rt, c0, width):
             return prm_t[:, rt * N + c0 : rt * N + c0 + width]
@@ -235,12 +247,6 @@ def tile_mix_lorab_sgd_kernel(tc, x, dn, hs_words, hs_scales, dy0, dy1, prm, out
             nc.vector.scalar_tensor_tensor(
                 out=dst, in0=acc[key][:, :width], scalar=STEP, in1=dst, op0=ALU.mult, op1=ALU.add
             )
-
-        part = {}
-
-        def scalar_drain(key):
-            part[key] = keep.tile([P, BLK], F32, name="part%d%d" % key)
-            nc.scalar.mul(out=part[key][:], in_=acc[key][:], mul=STEP)
 
         def gpsimd_finish(key):
             dst = result(key[0], key[1] * BLK, BLK)
@@ -254,29 +260,31 @@ def tile_mix_lorab_sgd_kernel(tc, x, dn, hs_words, hs_scales, dy0, dy1, prm, out
         dy_g = [staged("dy_g3%d" % nb) for nb in range(N_BLOCKS)]
         halves = [dy_g[0][:, u * HALF : (u + 1) * HALF, :] for u in range(2)]
         for u in range(2):
-            copy_columns(halves[u], 3, u * HALF, V_COLS_LAST[0])
-        deal_hs(1)
+            copy_columns(halves[u], 3, u * HALF, V_COLS_HALF)
         for u in range(2):
             quantize(halves[u], dy_q[3], u * HALF, E5M2)
             for key in in_block(0):
                 db_pass(key, 3, u)
-        copy_block(dy_g[1], 3, 1, V_COLS_LAST[1])
-        copy_block(dy_g[2], 3, 2, V_COLS_LAST[2])
-        quantize_block(dy_g[1], 3, 1, in_block(1))
-        quantize_block(dy_g[2], 3, 2, in_block(2))
+        for nb in (1, 2):
+            copy_columns(dy_g[nb][:], 3, nb * BLK, V_COLS_LAST)
+        for nb in (1, 2):
+            quantize_block(dy_g[nb], 3, nb)
         for rt in range(R_TILES):
             scalar_drain((rt, 0))
-        for bank, key in enumerate(late[:3]):
-            late_tile(key, bank)
-        late_tile((3, 2, 0), 3)
+        late_tile((2, 1), 0)
+        late_tile((2, 2), 1)
+        acc[parked] = bank_tile(2, "late2")
+        db_pass(parked, 3, first=3)
+        late_tile((3, 1), 3)
+        out_rows = by_pass(out)[:, 0, :]
         for rt in range(R_TILES):
             gpsimd_finish((rt, 0))
-            vector_finish((rt, 1))
-            if rt == 0:
-                late_tile((3, 2, 1), 4)
             if rt < 3:
+                vector_finish((rt, 1))
                 vector_finish((rt, 2))
             else:
-                for u in range(2):
-                    vector_finish((rt, 2, u))
-            (nc.sync, nc.scalar)[rt % 2].dma_start(out=runs(out)[:, rt * N : (rt + 1) * N], in_=result(rt, 0, N))
+                vector_finish(parked)
+                vector_finish((rt, 1))
+                dst = result(parked[0], parked[1] * BLK, BLK)
+                nc.vector.tensor_tensor(out=dst, in0=part[parked][:], in1=dst, op=ALU.add)
+            (nc.sync, nc.scalar)[rt % 2].dma_start(out=out_rows[:, rt * N : (rt + 1) * N], in_=result(rt, 0, N))

@@ -287,4 +287,4 @@ def tile_mix_lorab_sgd_kernel(tc, x, dn, hs_words, hs_scales, dy0, dy1, prm, out
                 vector_finish((rt, 1))
                 dst = result(parked[0], parked[1] * BLK, BLK)
                 nc.vector.tensor_tensor(out=dst, in0=part[parked][:], in1=dst, op=ALU.add)
-            (nc.sync, nc.scalar)[rt % 2].dma_start(out=out_rows[:, rt * N : (rt + 1) * N], in_=result(rt, 0, N))
+            nc.sync.dma_start(out=out_rows[:, rt * N : (rt + 1) * N], in_=result(rt, 0, N))

@@ -91,7 +91,7 @@ def tile_mix_lorab_sgd_kernel(tc, x, dn, hs_words, hs_scales, dy0, dy1, prm, out
         prm_t = keep.tile([P, R_TILES * N], F32, name="prm_t", align_bytes=256)
         sc_words = sc_in[:].bitcast(I32)
 
-        nc.gpsimd.memset(sc_words, 0)
+        nc.vector.memset(sc_words, 0)
         x_raw = load_passes(x, "x_raw", "first")
         nc.scalar.dma_start(out=hs_in[:].bitcast(I32), in_=hs_words.rearrange("a p c -> p a c").bitcast(I32))
         sc_rows = hs_scales.rearrange("a (h u j) n -> u j (a h) n", u=2, j=4).bitcast(I32)
@@ -146,43 +146,29 @@ def tile_mix_lorab_sgd_kernel(tc, x, dn, hs_words, hs_scales, dy0, dy1, prm, out
             sc_in[:, 1:5:2, :].rearrange("p a (m t) -> p a t m", t=PACK),
         )
 
-        def h_products(b):
-            banks = []
-            for rt in range(R_TILES):
-                bank = bank_tile(b * R_TILES + rt, "h_bank%d%d" % (b, rt))
-                for j in range(PACK):
-                    t0 = b * BLK + j * P
-                    for a in range(2):
-                        nc.tensor.matmul_mx(
-                            out=bank[:, j * P : (j + 1) * P],
-                            lhsT=x_q[a][0][:, t0 : t0 + P].bitcast(E4M3),
-                            lhsT_scale=x_q[a][1][:, t0 : t0 + P],
-                            rhs=dn_q[a][0][:, rt * P : (rt + 1) * P].bitcast(E4M3),
-                            rhs_scale=dn_q[a][1][:, rt * P : (rt + 1) * P],
-                            start=(a == 0),
-                            stop=(a == 1),
-                        )
-                banks.append(bank)
-            return banks
-
-        h_banks = [h_products(b) for b in range(2)]
+        h_rows = [keep.tile([P, PACK, R], BF16, name="h_rows%d" % b, align_bytes=64) for b in range(2)]
         for b in range(2):
-            h_g = staged("h_g%d" % b)
-            for rt in range(R_TILES):
-                copies[rt % 2](
-                    h_g[:, rt * P : (rt + 1) * P, :], h_banks[b][rt][:].rearrange("p (j r) -> p r j", j=PACK)
-                )
-            quantize(h_g[:], h_q[b], 0, E4M3)
+            for j in range(PACK):
+                bank = bank_tile(b * PACK + j, "h_bank%d%d" % (b, j))
+                t0 = b * BLK + j * P
+                for a in range(2):
+                    nc.tensor.matmul_mx(
+                        out=bank[:],
+                        lhsT=x_q[a][0][:, t0 : t0 + P].bitcast(E4M3),
+                        lhsT_scale=x_q[a][1][:, t0 : t0 + P],
+                        rhs=dn_q[a][0][:].bitcast(E4M3),
+                        rhs_scale=dn_q[a][1][:],
+                        start=(a == 0),
+                        stop=(a == 1),
+                    )
+                scalar_copy(h_rows[b][:, j, :], bank[:])
 
         acc = {}
 
         def db_pass(key, g, half=None, first=0, final=3):
-            rt, nb = key[:2]
-            c0, width = (nb * BLK, BLK) if len(key) == 2 else (nb * BLK + key[2] * HALF, HALF)
-            p0 = 0
-            if half is not None:
-                p0, width = half * HALF, HALF
-                c0 = c0 + p0
+            rt, nb = key
+            p0, width = (0, BLK) if half is None else (half * HALF, HALF)
+            c0 = nb * BLK + p0
             if g < 2:
                 lhsT = h_q[g][0][:, P * rt : P * (rt + 1)].bitcast(E4M3)
                 lhsT_scale = h_q[g][1][:, P * rt : P * (rt + 1)]
@@ -199,39 +185,45 @@ def tile_mix_lorab_sgd_kernel(tc, x, dn, hs_words, hs_scales, dy0, dy1, prm, out
                 stop=(g == final and half != 0),
             )
 
+        def dy_cols(g, c0, c1):
+            return dy_raw[g][:, :, c0:c1]
+
         def copy_columns(dst, g, c0, v_cols):
             width = dst.shape[1]
-            interleave(vector_copy, dst[:, :v_cols, :], dy_raw[g][:, :, c0 : c0 + v_cols])
-            interleave(scalar_copy, dst[:, v_cols:, :], dy_raw[g][:, :, c0 + v_cols : c0 + width])
+            interleave(vector_copy, dst[:, :v_cols, :], dy_cols(g, c0, c0 + v_cols))
+            interleave(scalar_copy, dst[:, v_cols:, :], dy_cols(g, c0 + v_cols, c0 + width))
 
         parked, successor = (3, 2), (1, 2)
         resident = [(rt, 0) for rt in range(R_TILES)] + [(0, 1), (1, 1), (0, 2), parked]
+        late = [(2, 1), (2, 2), parked, (3, 1)]
         for i, key in enumerate(resident):
             acc[key] = bank_tile(i, "acc%d%d" % key)
 
-        def in_block(nb):
-            return [key for key in resident if key[1] == nb]
+        def block_passes(g, nb, half=None):
+            for key in resident:
+                if key[1] == nb:
+                    db_pass(key, g, half, final=2 if key == parked else 3)
 
         def quantize_block(src, g, nb):
             quantize(src[:], dy_q[g], nb * BLK, E5M2)
-            for key in in_block(nb):
-                db_pass(key, g, final=2 if key == parked else 3)
+            block_passes(g, nb)
 
-        part = {}
+        h_g = [staged("h_g%d" % b) for b in range(2)]
+        for b in range(2):
+            interleave(vector_copy, h_g[b][:], h_rows[b][:])
+        for b in range(2):
+            quantize(h_g[b][:], h_q[b], 0, E4M3)
 
-        def scalar_drain(key):
-            part[key] = keep.tile([P, BLK], F32, name="part%d%d" % key)
-            nc.scalar.mul(out=part[key][:], in_=acc[key][:], mul=STEP)
-
-        steps = [(g, nb) for g in range(3) for nb in reversed(range(N_BLOCKS))]
         before = None
-        for g, nb in steps:
-            dy_g = staged("dy_g%d%d" % (g, nb))
-            copy_columns(dy_g[:], g, nb * BLK, V_COLS)
-            if before is not None:
-                quantize_block(*before)
-            before = (dy_g, g, nb)
-        scalar_drain(parked)
+        for g in range(3):
+            for nb in reversed(range(N_BLOCKS)):
+                dy_g = staged("dy_g%d%d" % (g, nb))
+                copy_columns(dy_g[:], g, nb * BLK, V_COLS)
+                if before is not None:
+                    quantize_block(*before)
+                before = (dy_g, g, nb)
+        early_sum = keep.tile([P, BLK], F32, name="early_sum")
+        nc.scalar.mul(out=early_sum[:], in_=acc[parked][:], mul=STEP)
         quantize_block(*before)
         resident[-1:] = [successor]
         acc[successor] = bank_tile(len(resident) - 1, "acc%d%d" % successor)
@@ -241,50 +233,42 @@ def tile_mix_lorab_sgd_kernel(tc, x, dn, hs_words, hs_scales, dy0, dy1, prm, out
         def result(rt, c0, width):
             return prm_t[:, rt * N + c0 : rt * N + c0 + width]
 
-        def vector_finish(key):
-            c0, width = (key[1] * BLK, BLK) if len(key) == 2 else (key[1] * BLK + key[2] * HALF, HALF)
-            dst = result(key[0], c0, width)
-            nc.vector.scalar_tensor_tensor(
-                out=dst, in0=acc[key][:, :width], scalar=STEP, in1=dst, op0=ALU.mult, op1=ALU.add
-            )
-
-        def gpsimd_finish(key):
+        def finish(key):
             dst = result(key[0], key[1] * BLK, BLK)
-            nc.gpsimd.tensor_tensor(out=dst, in0=part[key][:], in1=dst, op=ALU.add)
+            nc.vector.scalar_tensor_tensor(out=dst, in0=acc[key][:], scalar=STEP, in1=dst, op0=ALU.mult, op1=ALU.add)
 
-        def late_tile(key, bank):
-            acc[key] = bank_tile(bank, "late%d" % bank)
-            for g in range(4):
-                db_pass(key, g)
-
-        dy_g = [staged("dy_g3%d" % nb) for nb in range(N_BLOCKS)]
-        halves = [dy_g[0][:, u * HALF : (u + 1) * HALF, :] for u in range(2)]
+        last_g = [staged("dy_g3%d" % nb) for nb in range(N_BLOCKS)]
+        halves = [last_g[0][:, u * HALF : (u + 1) * HALF, :] for u in range(2)]
         for u in range(2):
             copy_columns(halves[u], 3, u * HALF, V_COLS_HALF)
         for u in range(2):
             quantize(halves[u], dy_q[3], u * HALF, E5M2)
-            for key in in_block(0):
-                db_pass(key, 3, u)
+            block_passes(3, 0, u)
         for nb in (1, 2):
-            copy_columns(dy_g[nb][:], 3, nb * BLK, V_COLS_LAST)
-        for nb in (1, 2):
-            quantize_block(dy_g[nb], 3, nb)
+            copy_columns(last_g[nb][:], 3, nb * BLK, V_COLS_LAST)
+        quantize_block(last_g[1], 3, 1)
+        quantize_block(last_g[2], 3, 2)
+
+        parts = []
         for rt in range(R_TILES):
-            scalar_drain((rt, 0))
-        late_tile((2, 1), 0)
-        late_tile((2, 2), 1)
-        acc[parked] = bank_tile(2, "late2")
-        db_pass(parked, 3, first=3)
-        late_tile((3, 1), 3)
+            part = stage.tile([P, BLK], F32, name="part%d" % rt, tag="stage", align_bytes=64)
+            nc.scalar.mul(out=part[:], in_=acc[rt, 0][:], mul=STEP)
+            parts.append(part)
+            acc[late[rt]] = bank_tile(rt, "late%d" % rt)
+            first = 3 if late[rt] == parked else 0
+            for g in range(first, 4):
+                db_pass(late[rt], g, first=first)
+
         out_rows = by_pass(out)[:, 0, :]
         for rt in range(R_TILES):
-            gpsimd_finish((rt, 0))
+            dst = result(rt, 0, BLK)
+            nc.gpsimd.tensor_tensor(out=dst, in0=parts[rt][:], in1=dst, op=ALU.add)
             if rt < 3:
-                vector_finish((rt, 1))
-                vector_finish((rt, 2))
+                finish((rt, 1))
+                finish((rt, 2))
             else:
-                vector_finish(parked)
-                vector_finish((rt, 1))
+                finish(parked)
+                finish((rt, 1))
                 dst = result(parked[0], parked[1] * BLK, BLK)
-                nc.vector.tensor_tensor(out=dst, in0=part[parked][:], in1=dst, op=ALU.add)
+                nc.vector.tensor_tensor(out=dst, in0=early_sum[:], in1=dst, op=ALU.add)
             nc.sync.dma_start(out=out_rows[:, rt * N : (rt + 1) * N], in_=result(rt, 0, N))

@@ -28,7 +28,7 @@ QUAD = 32
 V_COLS = 256
 V_COLS_HALF = 144
 V_COLS_LAST = 272
-PRM_LOADS = 3
+PRM_LOADS = 2
 
 
 def tile_mix_lorab_sgd_kernel(tc, x, dn, hs_words, hs_scales, dy0, dy1, prm, out):
@@ -195,7 +195,7 @@ def tile_mix_lorab_sgd_kernel(tc, x, dn, hs_words, hs_scales, dy0, dy1, prm, out
 
         parked, successor = (3, 2), (1, 2)
         resident = [(rt, 0) for rt in range(R_TILES)] + [(0, 1), (1, 1), (0, 2), parked]
-        late = [(2, 1), (2, 2), parked, (3, 1)]
+        late = [(2, 1), parked, (2, 2), (3, 1)]
         for i, key in enumerate(resident):
             acc[key] = bank_tile(i, "acc%d%d" % key)
 
@@ -249,26 +249,30 @@ def tile_mix_lorab_sgd_kernel(tc, x, dn, hs_words, hs_scales, dy0, dy1, prm, out
         quantize_block(last_g[1], 3, 1)
         quantize_block(last_g[2], 3, 2)
 
-        parts = []
-        for rt in range(R_TILES):
-            part = stage.tile([P, BLK], F32, name="part%d" % rt, tag="stage", align_bytes=64)
-            nc.scalar.mul(out=part[:], in_=acc[rt, 0][:], mul=STEP)
-            parts.append(part)
-            acc[late[rt]] = bank_tile(rt, "late%d" % rt)
-            first = 3 if late[rt] == parked else 0
+        def late_tile(key, bank):
+            acc[key] = bank_tile(bank, "late%d" % bank)
+            first = 3 if key == parked else 0
             for g in range(first, 4):
-                db_pass(late[rt], g, first=first)
+                db_pass(key, g, first=first)
+
+        part = {parked: early_sum}
+        for rt in range(R_TILES - 1):
+            part[rt, 0] = stage.tile([P, BLK], F32, name="part%d" % rt, tag="stage", align_bytes=64)
+            nc.scalar.mul(out=part[rt, 0][:], in_=acc[rt, 0][:], mul=STEP)
+            late_tile(late[rt], rt)
 
         out_rows = by_pass(out)[:, 0, :]
         for rt in range(R_TILES):
-            dst = result(rt, 0, BLK)
-            nc.gpsimd.tensor_tensor(out=dst, in0=parts[rt][:], in1=dst, op=ALU.add)
-            if rt < 3:
-                finish((rt, 1))
-                finish((rt, 2))
-            else:
-                finish(parked)
-                finish((rt, 1))
-                dst = result(parked[0], parked[1] * BLK, BLK)
-                nc.vector.tensor_tensor(out=dst, in0=early_sum[:], in1=dst, op=ALU.add)
+            for nb in range(N_BLOCKS):
+                if (rt, nb) in part:
+                    dst = result(rt, nb * BLK, BLK)
+                    nc.gpsimd.tensor_tensor(out=dst, in0=part[rt, nb][:], in1=dst, op=ALU.add)
+                else:
+                    finish((rt, nb))
+            if rt == 0:
+                late_tile(late[-1], R_TILES)
+            if rt == 1:
+                nc.vector.scalar_tensor_tensor(
+                    out=early_sum[:], in0=acc[parked][:], scalar=STEP, in1=early_sum[:], op0=ALU.mult, op1=ALU.add
+                )
             nc.sync.dma_start(out=out_rows[:, rt * N : (rt + 1) * N], in_=result(rt, 0, N))

@@ -29,6 +29,7 @@ V_COLS = 256
 V_COLS_HALF = 144
 V_COLS_LAST = 272
 PRM_LOADS = 2
+STORE_ENDS = (2, 6, 8, 12)
 
 
 def tile_mix_lorab_sgd_kernel(tc, x, dn, hs_words, hs_scales, dy0, dy1, prm, out):
@@ -262,17 +263,21 @@ def tile_mix_lorab_sgd_kernel(tc, x, dn, hs_words, hs_scales, dy0, dy1, prm, out
             late_tile(late[rt], rt)
 
         out_rows = by_pass(out)[:, 0, :]
-        for rt in range(R_TILES):
-            for nb in range(N_BLOCKS):
-                if (rt, nb) in part:
-                    dst = result(rt, nb * BLK, BLK)
-                    nc.gpsimd.tensor_tensor(out=dst, in0=part[rt, nb][:], in1=dst, op=ALU.add)
-                else:
-                    finish((rt, nb))
-            if rt == 0:
+        stored = 0
+        for i in range(R_TILES * N_BLOCKS):
+            key = divmod(i, N_BLOCKS)
+            if key in part:
+                dst = result(key[0], key[1] * BLK, BLK)
+                nc.gpsimd.tensor_tensor(out=dst, in0=part[key][:], in1=dst, op=ALU.add)
+            else:
+                finish(key)
+            if key == (0, 1):
                 late_tile(late[-1], R_TILES)
-            if rt == 1:
+            if key == successor:
                 nc.vector.scalar_tensor_tensor(
                     out=early_sum[:], in0=acc[parked][:], scalar=STEP, in1=early_sum[:], op0=ALU.mult, op1=ALU.add
                 )
-            nc.sync.dma_start(out=out_rows[:, rt * N : (rt + 1) * N], in_=result(rt, 0, N))
+            if i + 1 in STORE_ENDS:
+                cols = slice(stored * BLK, (i + 1) * BLK)
+                nc.sync.dma_start(out=out_rows[:, cols], in_=prm_t[:, cols])
+                stored = i + 1

@@ -27,7 +27,7 @@ LINE = 8
 QUAD = 32
 V_COLS = 256
 V_COLS_HALF = 144
-V_COLS_LAST = 272
+V_COLS_LAST = 280
 PRM_LOADS = 2
 STORE_ENDS = (2, 6, 8, 12)
 
@@ -45,10 +45,12 @@ def tile_mix_lorab_sgd_kernel(tc, x, dn, hs_words, hs_scales, dy0, dy1, prm, out
         def by_pass(rows):
             return rows.rearrange("(a p j) w -> p a (j w)", p=P, j=PACK)
 
-        def load_passes(src, name, slot):
+        def load_passes(src, name, slot, loads=1):
             view = by_pass(src)
             t = raw.tile(list(view.shape), F32, name=name, tag=slot, align_bytes=256)
-            nc.sync.dma_start(out=t[:], in_=view)
+            step = view.shape[1] // loads
+            for a in range(0, view.shape[1], step):
+                nc.sync.dma_start(out=t[:, a : a + step, :], in_=view[:, a : a + step, :])
             return [t[:, a, :].rearrange("p (j w) -> p j w", j=PACK) for a in range(view.shape[1])]
 
         def planes(name, width):
@@ -93,7 +95,7 @@ def tile_mix_lorab_sgd_kernel(tc, x, dn, hs_words, hs_scales, dy0, dy1, prm, out
         sc_words = sc_in[:].bitcast(I32)
 
         nc.vector.memset(sc_words, 0)
-        x_raw = load_passes(x, "x_raw", "first")
+        x_raw = load_passes(x, "x_raw", "first", loads=2)
         nc.scalar.dma_start(out=hs_in[:].bitcast(I32), in_=hs_words.rearrange("a p c -> p a c").bitcast(I32))
         sc_rows = hs_scales.rearrange("a (h u j) n -> u j (a h) n", u=2, j=4).bitcast(I32)
         nc.sync.dma_start(out=sc_words[0:4, 1:5, :], in_=sc_rows[0])
@@ -122,12 +124,7 @@ def tile_mix_lorab_sgd_kernel(tc, x, dn, hs_words, hs_scales, dy0, dy1, prm, out
                 quantize(x_g[a, b][:], x_q[a], b * BLK, E4M3)
 
         dy_raw.extend(load_passes(dy0[: P * PACK, :], "dy0_raw0", "first"))
-        last = raw.tile([P, PACK * N], F32, name="dy0_raw1", tag="last", align_bytes=256)
-        last_rows = by_pass(dy0)[:, 1, :]
-        cut = (PACK - 1) * N + BLK
-        nc.sync.dma_start(out=last[:, :cut], in_=last_rows[:, :cut])
-        nc.sync.dma_start(out=last[:, cut:], in_=last_rows[:, cut:])
-        dy_raw.append(last[:].rearrange("p (j w) -> p j w", j=PACK))
+        dy_raw.extend(load_passes(dy0[P * PACK :, :], "dy0_raw1", "last"))
         prm_rows = by_pass(prm)[:, 0, :]
         third = R_TILES * N // PRM_LOADS
         for c0 in range(0, R_TILES * N, third):

@@ -29,7 +29,7 @@ V_COLS = 256
 V_COLS_HALF = 144
 V_COLS_LAST = 280
 PRM_LOADS = 2
-STORE_ENDS = (2, 6, 8, 12)
+STORE_ENDS = (3 * BLK + P, 7 * BLK, R_TILES * N)
 
 
 def tile_mix_lorab_sgd_kernel(tc, x, dn, hs_words, hs_scales, dy0, dy1, prm, out):
@@ -100,7 +100,7 @@ def tile_mix_lorab_sgd_kernel(tc, x, dn, hs_words, hs_scales, dy0, dy1, prm, out
         sc_rows = hs_scales.rearrange("a (h u j) n -> u j (a h) n", u=2, j=4).bitcast(I32)
         nc.sync.dma_start(out=sc_words[0:4, 1:5, :], in_=sc_rows[0])
         nc.sync.dma_start(out=sc_words[3 * QUAD : 3 * QUAD + 4, 0:4, :], in_=sc_rows[1])
-        dn_raw = load_passes(dn, "dn_raw", "dn")
+        dn_raw = load_passes(dn, "dn_raw", "dn", loads=2)
         dy_raw = load_passes(dy1, "dy1_raw", "dy1")
 
         for a in range(2):
@@ -193,7 +193,6 @@ def tile_mix_lorab_sgd_kernel(tc, x, dn, hs_words, hs_scales, dy0, dy1, prm, out
 
         parked, successor = (3, 2), (1, 2)
         resident = [(rt, 0) for rt in range(R_TILES)] + [(0, 1), (1, 1), (0, 2), parked]
-        late = [(2, 1), parked, (2, 2), (3, 1)]
         for i, key in enumerate(resident):
             acc[key] = bank_tile(i, "acc%d%d" % key)
 
@@ -231,9 +230,11 @@ def tile_mix_lorab_sgd_kernel(tc, x, dn, hs_words, hs_scales, dy0, dy1, prm, out
         def result(rt, c0, width):
             return prm_t[:, rt * N + c0 : rt * N + c0 + width]
 
-        def finish(key):
-            dst = result(key[0], key[1] * BLK, BLK)
-            nc.vector.scalar_tensor_tensor(out=dst, in0=acc[key][:], scalar=STEP, in1=dst, op0=ALU.mult, op1=ALU.add)
+        def finish(key, width=BLK):
+            dst = result(key[0], key[1] * BLK, width)
+            nc.vector.scalar_tensor_tensor(
+                out=dst, in0=acc[key][:, :width], scalar=STEP, in1=dst, op0=ALU.mult, op1=ALU.add
+            )
 
         last_g = [staged("dy_g3%d" % nb) for nb in range(N_BLOCKS)]
         halves = [last_g[0][:, u * HALF : (u + 1) * HALF, :] for u in range(2)]
@@ -253,28 +254,37 @@ def tile_mix_lorab_sgd_kernel(tc, x, dn, hs_words, hs_scales, dy0, dy1, prm, out
             for g in range(first, 4):
                 db_pass(key, g, first=first)
 
-        part = {parked: early_sum}
-        for rt in range(R_TILES - 1):
-            part[rt, 0] = stage.tile([P, BLK], F32, name="part%d" % rt, tag="stage", align_bytes=64)
-            nc.scalar.mul(out=part[rt, 0][:], in_=acc[rt, 0][:], mul=STEP)
-            late_tile(late[rt], rt)
+        def drain(key, c0=0):
+            part = stage.tile([P, BLK], F32, name="part%d%d" % key, tag="stage", align_bytes=64)
+            nc.scalar.mul(out=part[:, c0:], in_=acc[key][:, c0:], mul=STEP)
+            return part[:, c0:]
+
+        def add(dst, part):
+            nc.gpsimd.tensor_tensor(out=dst, in0=part, in1=dst, op=ALU.add)
 
         out_rows = by_pass(out)[:, 0, :]
-        stored = 0
-        for i in range(R_TILES * N_BLOCKS):
-            key = divmod(i, N_BLOCKS)
-            if key in part:
-                dst = result(key[0], key[1] * BLK, BLK)
-                nc.gpsimd.tensor_tensor(out=dst, in0=part[key][:], in1=dst, op=ALU.add)
-            else:
-                finish(key)
-            if key == (0, 1):
-                late_tile(late[-1], R_TILES)
-            if key == successor:
-                nc.vector.scalar_tensor_tensor(
-                    out=early_sum[:], in0=acc[parked][:], scalar=STEP, in1=early_sum[:], op0=ALU.mult, op1=ALU.add
-                )
-            if i + 1 in STORE_ENDS:
-                cols = slice(stored * BLK, (i + 1) * BLK)
-                nc.sync.dma_start(out=out_rows[:, cols], in_=prm_t[:, cols])
-                stored = i + 1
+
+        def store(i):
+            cols = slice(STORE_ENDS[i - 1] if i else 0, STORE_ENDS[i])
+            nc.sync.dma_start(out=out_rows[:, cols], in_=prm_t[:, cols])
+
+        add(result(0, 0, BLK), drain((0, 0)))
+        add(result(1, P, BLK - P), drain((1, 0), P))
+        last_rows = drain((3, 0))
+        late_tile(parked, 0)
+        add(early_sum[:], drain(parked))
+        finish((0, 1))
+        late_tile((2, 1), 4)
+        late_tile((2, 2), 3)
+        finish((0, 2))
+        late_tile((3, 1), 6)
+        finish((1, 0), P)
+        store(0)
+        for key in ((1, 1), (1, 2), (2, 0)):
+            finish(key)
+        store(1)
+        add(result(3, 0, BLK), last_rows)
+        add(result(parked[0], parked[1] * BLK, BLK), early_sum[:])
+        for key in ((2, 1), (2, 2), (3, 1)):
+            finish(key)
+        store(2)

@@ -270,21 +270,23 @@ def tile_mix_lorab_sgd_kernel(tc, x, dn, hs_words, hs_scales, dy0, dy1, prm, out
 
         add(result(0, 0, BLK), drain((0, 0)))
         add(result(1, P, BLK - P), drain((1, 0), P))
-        last_rows = drain((3, 0))
+        last_rows = drain((3, 0), HALF)
         late_tile(parked, 0)
         add(early_sum[:], drain(parked))
         finish((0, 1))
         late_tile((2, 1), 4)
-        late_tile((2, 2), 3)
         finish((0, 2))
-        late_tile((3, 1), 6)
+        late_tile((2, 2), 6)
         finish((1, 0), P)
+        late_tile((3, 1), 1)
         store(0)
         for key in ((1, 1), (1, 2), (2, 0)):
             finish(key)
         store(1)
-        add(result(3, 0, BLK), last_rows)
+        add(result(3, HALF, HALF), last_rows)
         add(result(parked[0], parked[1] * BLK, BLK), early_sum[:])
-        for key in ((2, 1), (2, 2), (3, 1)):
-            finish(key)
+        finish((2, 1))
+        finish((2, 2))
+        finish((3, 0), HALF)
+        finish((3, 1))
         store(2)

from contextlib import ExitStack

import concourse.mybir as mybir

K, O, T, R, N = 1024, 1024, 1024, 512, 1536
FLOPS = 2 * K * T * R + 2 * (O + T) * R * N
STEP = -0.0625

F32 = mybir.dt.float32
BF16 = mybir.dt.bfloat16
I32 = mybir.dt.int32
U32 = mybir.dt.uint32
U16 = mybir.dt.uint16
U8 = mybir.dt.uint8
E4M3 = mybir.dt.float8_e4m3fn_x4
E5M2 = mybir.dt.float8_e5m2_x4
E2M1 = mybir.dt.float4_e2m1fn_x4
ALU = mybir.AluOpType

P = 128
PACK = 4
BLK = 512
HALF = BLK // 2
N_BLOCKS = N // BLK
R_TILES = R // P
LINE = 8
QUAD = 32
V_COLS = 256
V_COLS_HALF = 144
V_COLS_LAST = 280
PRM_LOADS = 2
STORE_ENDS = (3 * BLK + P, 7 * BLK, R_TILES * N)


def tile_mix_lorab_sgd_kernel(tc, x, dn, hs_words, hs_scales, dy0, dy1, prm, out):
    nc = tc.nc

    with ExitStack() as ctx:
        raw = ctx.enter_context(tc.tile_pool(name="raw", bufs=1))
        keep = ctx.enter_context(tc.tile_pool(name="keep", bufs=1))
        stage = ctx.enter_context(tc.tile_pool(name="stage", bufs=6))
        psum = ctx.enter_context(tc.psum_pool(name="psum", bufs=1))
        ctx.enter_context(tc.manual_schedule())

        def by_pass(rows):
            return rows.rearrange("(a p j) w -> p a (j w)", p=P, j=PACK)

        def load_passes(src, name, slot, loads=1):
            view = by_pass(src)
            t = raw.tile(list(view.shape), F32, name=name, tag=slot, align_bytes=256)
            step = view.shape[1] // loads
            for a in range(0, view.shape[1], step):
                nc.sync.dma_start(out=t[:, a : a + step, :], in_=view[:, a : a + step, :])
            return [t[:, a, :].rearrange("p (j w) -> p j w", j=PACK) for a in range(view.shape[1])]

        def planes(name, width):
            codes = keep.tile([P, width], U32, name=name + "_codes", align_bytes=64)
            scales = keep.tile([P, width], U8, name=name + "_scales", align_bytes=64)
            return codes, scales

        def staged(name):
            return stage.tile([P, BLK, PACK], BF16, name=name, tag="stage", align_bytes=64)

        def vector_copy(dst, src):
            nc.vector.tensor_copy(out=dst, in_=src)

        def scalar_copy(dst, src):
            nc.scalar.copy(out=dst, in_=src)

        copies = (vector_copy, scalar_copy)

        def interleave(copy, dst, src):
            copy(dst.rearrange("p (c i) j -> p c j i", i=4), src.rearrange("p j (c i) -> p c j i", i=4))

        def interleave_dealt(copy, dst, src):
            copy(dst.rearrange("p (t m) j -> p m j t", t=PACK), src.rearrange("p j (m t) -> p m j t", t=PACK))

        def quantize(g, plane, col0, fmt):
            codes, scales = plane
            width = g.shape[1]
            nc.vector.quantize_mx(
                out=codes[:, col0 : col0 + width].bitcast(fmt),
                scales=scales[:, col0 : col0 + width],
                in_=g.rearrange("p w j -> p (w j)"),
            )

        def bank_tile(i, name):
            return psum.tile([P, BLK], F32, name=name, tag="bank%d" % i)

        sc_in = keep.tile([P, 5, R], U8, name="sc_in", align_bytes=256)
        hs_sc = keep.tile([P, 2, R], U8, name="hs_sc", align_bytes=64)
        hs_in = keep.tile([P, 2, 2 * R], U8, name="hs_in", align_bytes=256)
        hs_w = keep.tile([P, 2, 2 * R], U8, name="hs_w", align_bytes=64)
        prm_t = keep.tile([P, R_TILES * N], F32, name="prm_t", align_bytes=256)
        sc_words = sc_in[:].bitcast(I32)

        nc.vector.memset(sc_words, 0)
        x_raw = load_passes(x, "x_raw", "first", loads=2)
        nc.scalar.dma_start(out=hs_in[:].bitcast(I32), in_=hs_words.rearrange("a p c -> p a c").bitcast(I32))
        sc_rows = hs_scales.rearrange("a (h u j) n -> u j (a h) n", u=2, j=4).bitcast(I32)
        nc.sync.dma_start(out=sc_words[0:4, 1:5, :], in_=sc_rows[0])
        nc.sync.dma_start(out=sc_words[3 * QUAD : 3 * QUAD + 4, 0:4, :], in_=sc_rows[1])
        dn_raw = load_passes(dn, "dn_raw", "dn", loads=2)
        dy_raw = load_passes(dy1, "dy1_raw", "dy1")

        for a in range(2):
            scalar_copy(
                hs_w[:, a, :].bitcast(U16).rearrange("p (t c i) -> p c t i", t=PACK, i=LINE),
                hs_in[:, a, :].bitcast(U16).rearrange("p (c i t) -> p c t i", t=PACK, i=LINE),
            )

        x_q = [planes("x%d" % a, T) for a in range(2)]
        dn_q = [planes("dn%d" % a, R) for a in range(2)]
        h_q = [planes("h%d" % b, R) for b in range(2)]
        dy_q = [planes("dy%d" % g, N) for g in range(4)]

        x_g = {}
        for b in range(2):
            for a in range(2):
                x_g[a, b] = staged("x_g%d%d" % (a, b))
                interleave_dealt(copies[a], x_g[a, b][:], x_raw[a][:, :, b * BLK : (b + 1) * BLK])
        for b in range(2):
            for a in range(2):
                quantize(x_g[a, b][:], x_q[a], b * BLK, E4M3)

        dy_raw.extend(load_passes(dy0[: P * PACK, :], "dy0_raw0", "first"))
        dy_raw.extend(load_passes(dy0[P * PACK :, :], "dy0_raw1", "last"))
        prm_rows = by_pass(prm)[:, 0, :]
        third = R_TILES * N // PRM_LOADS
        for c0 in range(0, R_TILES * N, third):
            nc.sync.dma_start(out=prm_t[:, c0 : c0 + third], in_=prm_rows[:, c0 : c0 + third])

        dn_g = [staged("dn_g%d" % a) for a in range(2)]
        for a in range(2):
            interleave_dealt(copies[a], dn_g[a][:], dn_raw[a])
        for a in range(2):
            quantize(dn_g[a][:], dn_q[a], 0, E4M3)

        for a in range(2):
            vector_copy(sc_words[2 * QUAD : 2 * QUAD + 4, 1 + 2 * a, :], sc_words[0:4, 2 + 2 * a, :])
            vector_copy(sc_words[QUAD : 2 * QUAD, 1 + 2 * a, :], sc_words[3 * QUAD :, 2 * a, :])
        vector_copy(
            hs_sc[:].rearrange("p a (t m) -> p a t m", t=PACK),
            sc_in[:, 1:5:2, :].rearrange("p a (m t) -> p a t m", t=PACK),
        )

        h_rows = [keep.tile([P, PACK, R], BF16, name="h_rows%d" % b, align_bytes=64) for b in range(2)]
        for b in range(2):
            for j in range(PACK):
                bank = bank_tile(b * PACK + j, "h_bank%d%d" % (b, j))
                t0 = b * BLK + j * P
                for a in range(2):
                    nc.tensor.matmul_mx(
                        out=bank[:],
                        lhsT=x_q[a][0][:, t0 : t0 + P].bitcast(E4M3),
                        lhsT_scale=x_q[a][1][:, t0 : t0 + P],
                        rhs=dn_q[a][0][:].bitcast(E4M3),
                        rhs_scale=dn_q[a][1][:],
                        start=(a == 0),
                        stop=(a == 1),
                    )
                scalar_copy(h_rows[b][:, j, :], bank[:])

        acc = {}

        def db_pass(key, g, half=None, first=0, final=3):
            rt, nb = key
            p0, width = (0, BLK) if half is None else (half * HALF, HALF)
            c0 = nb * BLK + p0
            if g < 2:
                lhsT = h_q[g][0][:, P * rt : P * (rt + 1)].bitcast(E4M3)
                lhsT_scale = h_q[g][1][:, P * rt : P * (rt + 1)]
            else:
                lhsT = hs_w[:, g - 2, 2 * P * rt : 2 * P * (rt + 1)].bitcast(E2M1)
                lhsT_scale = hs_sc[:, g - 2, P * rt : P * (rt + 1)]
            nc.tensor.matmul_mx(
                out=acc[key][:, p0 : p0 + width],
                lhsT=lhsT,
                lhsT_scale=lhsT_scale,
                rhs=dy_q[g][0][:, c0 : c0 + width].bitcast(E5M2),
                rhs_scale=dy_q[g][1][:, c0 : c0 + width],
                start=(g == first),
                stop=(g == final and half != 0),
            )

        def dy_cols(g, c0, c1):
            return dy_raw[g][:, :, c0:c1]

        def copy_columns(dst, g, c0, v_cols):
            width = dst.shape[1]
            interleave(vector_copy, dst[:, :v_cols, :], dy_cols(g, c0, c0 + v_cols))
            interleave(scalar_copy, dst[:, v_cols:, :], dy_cols(g, c0 + v_cols, c0 + width))

        parked, successor = (3, 2), (1, 2)
        resident = [(rt, 0) for rt in range(R_TILES)] + [(0, 1), (1, 1), (0, 2), parked]
        for i, key in enumerate(resident):
            acc[key] = bank_tile(i, "acc%d%d" % key)

        def block_passes(g, nb, half=None):
            for key in resident:
                if key[1] == nb:
                    db_pass(key, g, half, final=2 if key == parked else 3)

        def quantize_block(src, g, nb):
            quantize(src[:], dy_q[g], nb * BLK, E5M2)
            block_passes(g, nb)

        h_g = [staged("h_g%d" % b) for b in range(2)]
        for b in range(2):
            interleave(vector_copy, h_g[b][:], h_rows[b][:])
        for b in range(2):
            quantize(h_g[b][:], h_q[b], 0, E4M3)

        before = None
        for g in range(3):
            for nb in reversed(range(N_BLOCKS)):
                dy_g = staged("dy_g%d%d" % (g, nb))
                copy_columns(dy_g[:], g, nb * BLK, V_COLS)
                if before is not None:
                    quantize_block(*before)
                before = (dy_g, g, nb)
        early_sum = keep.tile([P, BLK], F32, name="early_sum")
        nc.scalar.mul(out=early_sum[:], in_=acc[parked][:], mul=STEP)
        quantize_block(*before)
        resident[-1:] = [successor]
        acc[successor] = bank_tile(len(resident) - 1, "acc%d%d" % successor)
        for g in range(3):
            db_pass(successor, g)

        def result(rt, c0, width):
            return prm_t[:, rt * N + c0 : rt * N + c0 + width]

        def finish(key, width=BLK):
            dst = result(key[0], key[1] * BLK, width)
            nc.vector.scalar_tensor_tensor(
                out=dst, in0=acc[key][:, :width], scalar=STEP, in1=dst, op0=ALU.mult, op1=ALU.add
            )

        last_g = [staged("dy_g3%d" % nb) for nb in range(N_BLOCKS)]
        halves = [last_g[0][:, u * HALF : (u + 1) * HALF, :] for u in range(2)]
        for u in range(2):
            copy_columns(halves[u], 3, u * HALF, V_COLS_HALF)
        for u in range(2):
            quantize(halves[u], dy_q[3], u * HALF, E5M2)
            block_passes(3, 0, u)
        for nb in (1, 2):
            copy_columns(last_g[nb][:], 3, nb * BLK, V_COLS_LAST)
        quantize_block(last_g[1], 3, 1)
        quantize_block(last_g[2], 3, 2)

        def late_tile(key, bank):
            acc[key] = bank_tile(bank, "late%d" % bank)
            first = 3 if key == parked else 0
            for g in range(first, 4):
                db_pass(key, g, first=first)

        def drain(key, c0=0):
            part = stage.tile([P, BLK], F32, name="part%d%d" % key, tag="stage", align_bytes=64)
            nc.scalar.mul(out=part[:, c0:], in_=acc[key][:, c0:], mul=STEP)
            return part[:, c0:]

        def add(dst, part):
            nc.gpsimd.tensor_tensor(out=dst, in0=part, in1=dst, op=ALU.add)

        out_rows = by_pass(out)[:, 0, :]

        def store(i):
            cols = slice(STORE_ENDS[i - 1] if i else 0, STORE_ENDS[i])
            nc.sync.dma_start(out=out_rows[:, cols], in_=prm_t[:, cols])

        add(result(0, 0, BLK), drain((0, 0)))
        add(result(1, P, BLK - P), drain((1, 0), P))
        last_rows = drain((3, 0), HALF)
        late_tile(parked, 0)
        add(early_sum[:], drain(parked))
        finish((0, 1))
        late_tile((2, 1), 4)
        finish((0, 2))
        late_tile((2, 2), 6)
        finish((1, 0), P)
        late_tile((3, 1), 1)
        store(0)
        for key in ((1, 1), (1, 2), (2, 0)):
            finish(key)
        store(1)
        add(result(3, HALF, HALF), last_rows)
        add(result(parked[0], parked[1] * BLK, BLK), early_sum[:])
        finish((2, 1))
        finish((2, 2))
        finish((3, 0), HALF)
        finish((3, 1))
        store(2)
